import numpy as np, ml_dtypes
CORES = [23,119,17,113]
N = 4
import mx_ref
BF = ml_dtypes.bfloat16
def gcols(t, e):
    v = np.concatenate([t.reshape(8, 16, -1, 4), np.zeros((8, 16, 1, 4), BF)], axis=2)
    return np.ascontiguousarray(np.stack([v[g][:, e[g]] for g in range(8)])).reshape(128, -1)
def tile(rs):
    return np.stack(rs, axis=2).reshape(128, -1).astype(BF)
def pick(q, e):
    c = np.concatenate([q[0].reshape(128, -1, 4), np.zeros((128, 1, 4), np.uint8)], axis=1); s = np.concatenate([q[1], np.ones((16, 1), np.uint8)], axis=1)
    return (np.ascontiguousarray(c[:, e].reshape(128, -1)), np.ascontiguousarray(s[:, e]))
def join(*qs):
    return (np.concatenate([q[0] for q in qs], axis=1), np.concatenate([q[1] for q in qs], axis=1))
def put(q, e, v):
    c, s = q[0].reshape(128, -1, 4).copy(), q[1].copy(); c[:, e] = v[0].reshape(128, -1, 4); s[:, e] = v[1]
    return (c.reshape(128, -1), s)
def pk(c, s):
    return (np.ascontiguousarray(c), mx_ref.live(s))
def emit(q):
    return q[0], q[1]
def packed(v, rng):
    q = [mx_ref.quantize(np.ascontiguousarray(v[r])) for r in range(N)]
    return np.stack([a for a, b in q]), np.stack([mx_ref.plane(b, rng) for a, b in q])
def values_of_codes():
    e, c = np.zeros((128, 128, 4), np.float32), np.zeros((128, 2, 4), np.uint8)
    e[np.arange(128), np.arange(128), 0] = 1
    c[:127, :, 0] = np.arange(256).reshape(2, 128).T[:127]
    return mx_ref.matmul(mx_ref.quantize(e.reshape(128, 512).astype(BF)), (c.reshape(128, 8), np.full((16, 2), 127, np.uint8))).T.reshape(-1).astype(np.float64)
CODE_VALUE, SCALE_VALUE = values_of_codes(), 2.0 ** (np.arange(256) - 127.0)
def decode(q):
    return (CODE_VALUE[q[0]].reshape(16, 8, -1, 4) * SCALE_VALUE[q[1]][:, None, :, None] + 0.0).reshape(128, -1).astype(np.float32)
def f(rng, *shape):
    return mx_ref.flush((rng.standard_normal(shape, dtype=np.float32) * np.exp2(rng.integers(-2, 3, shape[:-1] + (1,)))).astype(BF))
def wide(rng, *shape, cols=0):
    v = rng.standard_normal(shape, dtype=np.float32) * np.exp2(rng.integers(-12, 13, shape)).astype(np.float32)
    if cols: v *= np.repeat(np.exp2(rng.integers(-cols, cols + 1, shape[:-2] + (1, shape[-1] // 4))) * (rng.random(shape[:-2] + (1, shape[-1] // 4)) > 0.0625), 4, axis=-1).astype(np.float32)
    return mx_ref.flush(v.astype(BF))
C, V, R = 320, 18, 3
STEP = [1, 2, 1]
def match(a, b):
    k = (np.arange(C)[:, None] + np.arange(-V, V + 1)) % C
    return np.argmin(np.abs(a[:, :, None] - b[:, k]), axis=2) - V
def inherit(d, e):
    place = np.arange(C)
    ok = np.take_along_axis(e, (place + d) % C, axis=1) == -d
    before = np.maximum.accumulate(np.where(ok, place, -1), axis=1)
    behind = np.minimum.accumulate(np.where(ok, place, C)[:, ::-1], axis=1)[:, ::-1]
    before, behind = np.where(before < 0, behind, before), np.where(behind == C, before, behind)
    z = np.concatenate([d, np.zeros((8, 1), int)], axis=1)
    return np.take_along_axis(z, before, axis=1), np.take_along_axis(z, behind, axis=1)
def big(v):
    v = v.astype(np.float32)
    v[np.abs(v) < np.float32(2.0 ** -16)] = 0
    return v.astype(BF)
def numbers_of(rng):
    return {"x": big(f(rng, N, 128, 4 * C)), "u": np.array(f(rng, N, 128, 512)), "v": np.array(f(rng, N, 128, 512))}
def weights(rng, still=[]):
    w = np.array(f(rng, N, 128, 2048)).reshape(N, 8, 16, 4, 8, 16, 4)
    for i in still:
        w[:, :, i] = 0
        w[:, :, :, :, :, i] = 0
    c, p = packed(w.reshape(N, 128, 2048), rng)
    return {"wc": c, "ws": p}
def digits(k, n):
    z = k[..., None] & (1 << np.arange(4 * n))
    return np.stack([z[..., 4 * i:4 * i + 4] for i in range(n)], axis=2)
def signs(rng):
    p = rng.permutation(8)
    m = (p // 2) ^ (p % 2 * (N - 1))
    c = np.array([[1.0 - 2 * (bin(r & int(k)).count("1") % 2) for k in m] for r in range(N)])
    return p // 2, c * rng.choice([-1.0, 1.0], 8)
def planted(case, rng):
    a, b = np.zeros(C, int), np.full(C, 100)
    if case < 3:
        a = rng.permutation(C)
        b = np.roll(a, [V, -V, int(rng.integers(-V, V + 1))][case])
    elif 3 < case < 7:
        n = C // (2 * V + 2)
        j = [np.array([0]), np.array([C - 1]), np.arange(n) * (2 * V + 2) + rng.integers(2 * V + 2)][case - 4]
        e = [np.array([-V]), np.array([V]), rng.permutation(np.concatenate([[-V, V], rng.integers(1 - V, V, n - 2)]))][case - 4]
        a[j] = 40
        b[(j + e) % C] = 50
    elif case == 7:
        a, b = rng.integers(0, 40, C), rng.integers(0, 40, C)
    return a, b
def setup_inputs(rng):
    return {**numbers_of(rng), **weights(rng)}
def setup_inputs_ties(rng):
    d = numbers_of(rng)
    x = d["x"].reshape(N, 8, 16, C, 4)
    u = d["u"].reshape(N, 8, 16, 128, 4)
    a = x[0][:, :8, :3].copy()
    a[:, :, 2] = 0
    e = int(rng.integers(N))
    for r in range(N):
        k = np.full(C, rng.integers(2)) if r in (e, e ^ STEP[R - 1]) else rng.permutation(C) % 3
        x[r][:, :8] = a[:, :, k]
    x[e ^ STEP[1]] = 0
    u[1:] = u[0]
    u[:, :, 8:, ::16] = 0
    return {"x": x.reshape(N, 128, 4 * C), "u": u.reshape(N, 128, 512), "v": d["v"], **weights(rng, range(8))}
def setup_inputs_near(rng):
    d = numbers_of(rng)
    o, c = signs(rng)
    x = d["x"].astype(np.float32).reshape(N, 8, 16, C, 4)
    u = d["u"].reshape(N, 128, 128, 4)
    size = np.where(o < 2, 2.0 ** -23, 2.0 ** -27)
    x[:, :, 0] = 0
    x[:, :, 8:] = 0
    x[:, :, 0, :, 0] = (c * (o < 2))[:, :, None]
    x[:, :, 8:10] = digits(rng.integers(0, 256, (N, 8, C)), 2) * size[:, None, None, None]
    x[:, :, 10, :, 0] = rng.integers(8, 16, (N, 8, C)) * (o == 3)[:, None] * 2.0 ** -30
    u[:, :, ::16] = 0
    for g in range(8):
        h, k = 16 * g, 1.0 if o[g] == 0 else 2.0 ** -30
        u[:, h, h, 0] = k
        u[:, h + 8:h + 10, h] = k
        u[:, h + 10, h, 0] = k
    return {"x": x.reshape(N, 128, 4 * C).astype(BF), "u": u.reshape(N, 128, 512), "v": d["v"], **weights(rng, [0, 8, 9, 10, 11, 12, 13, 14, 15])}
def setup_inputs_huge(rng):
    d = numbers_of(rng)
    o, c = signs(rng)
    n = np.stack([rng.permutation(513)[:C] for r in range(N)])
    i = np.argsort(rng.random((N, 512, C)), axis=1)
    x = (-2.0 ** 30 * np.where(i < n[:, None], 1.0, 0.875)).reshape(N, 128, 4, C).transpose(0, 1, 3, 2)
    u = d["u"].reshape(N, 128, 128, 4)
    u[:, :, ::16] = (2.0 ** 30 * c).astype(np.float32).astype(BF)[:, None, :, None]
    return {"x": np.ascontiguousarray(x).astype(np.float32).reshape(N, 128, 4 * C).astype(BF), "u": u.reshape(N, 128, 512), "v": d["v"], **weights(rng, range(16))}
def setup_inputs_lists(rng):
    d = numbers_of(rng)
    s = np.zeros((N, 8, C), int)
    for r in range(N):
        p = r ^ STEP[R - 1]
        if r < p:
            n = rng.permutation(8)
            for g in range(8): s[r, g], s[p, g] = planted(int(n[g]), rng)
    x = d["x"].astype(np.float32).reshape(N, 8, 16, C, 4)
    u = d["u"].reshape(N, 128, 128, 4)
    x[:, :, 8:] = 0
    x[:, :, 8:11] = digits(s, 3)
    u[:, :, ::16] = 0
    for h in range(0, 128, 16): u[:, h + 8:h + 11, h] = 1
    return {"x": x.reshape(N, 128, 4 * C).astype(BF), "u": u.reshape(N, 128, 512), "v": d["v"], **weights(rng, range(8, 16))}
def setup_inputs_spread(rng):
    d = setup_inputs(rng)
    d["x"] = big(wide(rng, N, 128, 4 * C, cols=6))
    return d
def check_inputs(d):
    b = []
    for k in ("x", "u", "v"):
        a = np.abs(d[k].astype(np.float32))
        if not (np.isfinite(a).all() and ((a == 0) | (a >= 2.0 ** -30) & (a <= 2.0 ** 30)).all()): b.append("a value of " + k)
    if ((d["wc"] & 0x7F) == 0x7F).any(): b.append("a code of wc that is no number")
    none, least, most = [emit(mx_ref.quantize(np.full((128, 16), k, np.float32).astype(BF)))[1][0, 0] for k in (0.0, 2.0 ** -30, 2.0 ** 30)]
    for r in range(N):
        s = mx_ref.live(d["ws"][r])
        if ((s != none) & ((s < least) | (s > most))).any(): b.append("a scale of ws")
        if ((s == none)[:, None, :, None] & ((d["wc"][r].reshape(16, 8, -1, 4) & 0x7F) != 0)).any(): b.append("a code of wc under the scale of zeros")
    return b
def reference(x, u, v, wc, ws):
    qu = [mx_ref.quantize(u[r]) for r in range(N)]
    lay = [pk(wc[r], ws[r]) for r in range(N)]
    now = [x[r] for r in range(N)]
    place = np.arange(C)
    y, od = np.zeros((N, 128, C), np.float32), np.zeros((N, 8, 2 * C), np.float32)
    oc, osc = np.zeros((N, 128, 4 * C), np.uint8), np.zeros((N, 16, C), np.uint8)
    for t in range(R):
        q = [mx_ref.quantize(now[r]) for r in range(N)]
        s = [mx_ref.matmul(qu[r], q[r])[::16] for r in range(N)]
        held = [decode(q[r]) for r in range(N)]
        d = [match(s[r], s[r ^ STEP[t]]) for r in range(N)]
        made = []
        for r in range(N):
            e = r ^ STEP[t]
            l, h = inherit(d[r], d[e])
            p = held[e].astype(BF)
            z = ((gcols(p, (place + l) % C).astype(np.float32) + gcols(p, (place + h) % C).astype(np.float32)) * np.float32(0.5)).astype(BF)
            qz = mx_ref.quantize(z)
            made.append(tile([np.maximum(mx_ref.matmul(pick(lay[r], np.arange(128 * b, 128 * b + 128)), qz), np.float32(0.0)) * np.float32(0.03125) + held[r][:, b::4] for b in range(4)]))
            od[r] = np.concatenate([l, h], axis=1)
        now = made
    for r in range(N):
        last = mx_ref.quantize(now[r])
        y[r] = mx_ref.matmul(mx_ref.quantize(v[r]), last)
        oc[r], osc[r] = emit(last)
    return {"y": y, "od": od, "oc": oc, "osc": osc}

@@ -1,0 +1,530 @@
+from concourse.mybir import dt, AluOpType, AxisListType, ActivationFunctionType
+
+C, V, R = 320, 18, 3
+STEP = [1, 2, 1]
+NT = C // 16
+KW = 2 * V + 1
+HT = NT // 2
+HK = HT * KW
+HC = C // 2
+CE = C + 2 * V
+PW = 368
+NKD = 9
+BIG = 1.0e29
+F32, BF, I32, U16, Q4, U8 = "float32", "bfloat16", "int32", "uint16", "float8_e4m3fn_x4", "uint8"
+
+_SB = {
+    "x0": (4 * CE, BF), "ut": (512, BF), "vt": (512, BF), "ones": (528, BF), "eb": (528, BF),
+    "qu": (128, Q4), "su": (128, U8), "qur": (128, Q4), "sur": (128, U8), "qv": (128, Q4), "sv": (128, U8),
+    "qw": (512, Q4), "sw": (512, U8), "qe": (512, Q4), "se": (512, U8), "qy": (C, Q4), "sy": (C, U8),
+    "xt": (4 * C, BF), "yt": (4 * C, BF), "hb": (4 * C, BF), "rl": (4 * C, F32), "psb": (4 * PW, BF),
+    "pj": (8, I32), "pf": (8, F32), "cl": (16, F32), "rp": (64, F32), "r16": (C, F32),
+    "mk": (C, F32), "nm": (C, F32), "sm": (C, F32), "sc": (C, F32), "t1": (32, F32), "t2": (64, F32),
+    "dd": (4 * HK, F32), "mm": (4 * HK, F32), "rs": (HK, F32), "kp": (HK, BF), "fl": (2 * HK, BF), "f2": (HK, BF),
+    "cs": (1248, BF), "t1b": (32, BF), "t2b": (64, BF), "cd": (64, F32), "r65": (64, F32),
+    "nd": (32, F32), "bi": (32, F32), "cb": (32, F32), "ex": (32, F32), "ks": (2 * HK, F32), "jk": (2 * HK, BF),
+    "ok": (32, F32), "kb": (48, F32), "ckb": (48, F32), "ky": (48, F32), "kk": (48, F32), "lo": (48, F32),
+    "zz": (128, F32), "cz": (128, F32), "zt": (128, F32), "fi": (48, I32), "lw": (48, I32),
+    "cc": (96, F32), "na": (48, F32), "off": (48, U16), "odt": (48, F32), "yo": (C, F32),
+    "lpi": (20, U16), "lu": (8, U16), "lrot": (4, U16), "lc1": (4, U16), "lc2": (4, U16), "lnr": (24, U16),
+    "lnf": (20, U16), "ldup": (4, U16), "lfin": (4, U16),
+    "k1": (64, F32), "k2": (64, F32), "k3": (128, F32), "k4": (64, F32), "k5": (64, I32), "k6": (64, F32),
+    "k7": (128, F32), "k9": (64, F32), "nn": (32, F32),
+}
+for _r in range(R + 1):
+    _SB["qn%d" % _r] = (PW, Q4)
+    _SB["sn%d" % _r] = (PW, U8)
+    _SB["qp%d" % _r] = (C, Q4)
+    _SB["sp%d" % _r] = (C, U8)
+for _r in range(R):
+    _SB["lq%d" % _r] = (CE, Q4)
+    _SB["ls%d" % _r] = (CE, U8)
+    _SB["ao%d" % _r] = (96, F32)
+    _SB["ap%d" % _r] = (96, F32)
+    _SB["wo%d" % _r] = (64, F32)
+    _SB["wp%d" % _r] = (64, F32)
+SCRATCH = {k: ("sbuf", [128, n], d) for k, (n, d) in _SB.items()}
+for _b in range(8):
+    SCRATCH["pb%d" % _b] = ("psum", [128, 512], F32)
+NDMA = 20
+SEMAPHORES = (["cv", "ca", "ct", "cg", "sent"] + ["dm%d" % k for k in range(NDMA)]
+              + ["%s%d" % (n, k) for k in range(R) for n in ("aw", "ax", "ab")])
+
+A = AluOpType
+AF = ActivationFunctionType
+
+
+def rank_program(g, core, T, topo):
+    rank = T.rank_of(core)
+    if rank is None:
+        return
+    eng = {"v": g.vector, "a": g.scalar, "t": g.tensor, "g": g, "s": g.sync}
+    csem = {"v": "cv", "a": "ca", "t": "ct", "g": "cg"}
+    count = {}
+    known = {q: {} for q in eng}
+    events = []
+    lastw = {}
+    reads = {}
+    bank = {}
+    ndma = [0]
+
+    def cols(v):
+        return range(v[1], v[2], v[3])
+
+    def W(name, a=0, b=None, s=1):
+        return (name, a, SCRATCH[name][1][1] if b is None else b, s)
+
+    def ap(v):
+        return T[v[0]][:, v[1]:v[2]] if v[3] == 1 else T[v[0]][:, v[1]:v[2]:v[3]]
+
+    def need(q, e):
+        sem, val_, clk = events[e][0], events[e][1], events[e][2]
+        if known[q].get(sem, 0) >= val_:
+            return
+        eng[q].wait_ge(T.sem[sem], val_)
+        for s, n in clk.items():
+            if known[q].get(s, 0) < n:
+                known[q][s] = n
+        known[q][sem] = val_
+
+    def order(q, rd, wr):
+        deps = set()
+        for v in rd:
+            lw_ = lastw.setdefault(v[0], {})
+            deps.update(lw_[c] for c in cols(v) if c in lw_)
+        for v in wr:
+            lw_ = lastw.setdefault(v[0], {})
+            rr = reads.setdefault(v[0], {})
+            for c in cols(v):
+                if c in lw_:
+                    deps.add(lw_[c])
+                deps.update(rr.get(c, ()))
+        for v in rd + wr:
+            if SCRATCH[v[0]][0] == "psum":
+                deps.update(e for e in bank.get(v[0], []) if events[e][3] != q)
+        for e in sorted(deps, reverse=True):
+            need(q, e)
+
+    def note(q, sem, n, rd, wr):
+        count[sem] = count.get(sem, 0) + n
+        e = len(events)
+        events.append((sem, count[sem], dict(known[q]) if q else {}, q))
+        for v in rd:
+            rr = reads.setdefault(v[0], {})
+            for c in cols(v):
+                rr.setdefault(c, []).append(e)
+        for v in wr:
+            lw_ = lastw.setdefault(v[0], {})
+            rr = reads.setdefault(v[0], {})
+            for c in cols(v):
+                lw_[c] = e
+                rr.pop(c, None)
+        for v in rd + wr:
+            if SCRATCH[v[0]][0] == "psum":
+                bank[v[0]] = [x for x in bank.get(v[0], []) if events[x][3] == q] + [e]
+        return e
+
+    def op(q, fn, rd, wr):
+        order(q, rd, wr)
+        fn().then_inc(T.sem[csem[q]], 1)
+        return note(q, csem[q], 1, rd, wr)
+
+    def dma(q, out, in_, rd, wr):
+        order(q, rd, wr)
+        sem = "dm%d" % ndma[0]
+        ndma[0] += 1
+        eng[q].dma_start(out, in_).then_inc(T.sem[sem], 16)
+        return note(q, sem, 16, rd, wr)
+
+    def views(*xs):
+        return [x for x in xs if isinstance(x, tuple)]
+
+    def val(x):
+        return ap(x) if isinstance(x, tuple) else x
+
+    def src(v, ind):
+        return ap(v) if ind is None else ap(v).indirect(ap(ind))
+
+    def cp(o, i, ind=None):
+        return op("v", lambda: g.vector.tensor_copy(ap(o), src(i, ind)), views(i, ind), [o])
+
+    def tt(o, a, b, f, ind=None):
+        return op("v", lambda: g.vector.tensor_tensor(ap(o), src(a, ind), ap(b), f), views(a, b, ind), [o])
+
+    def ts(o, a, s1, f1, s2=None, f2=None):
+        if f2 is None:
+            return op("v", lambda: g.vector.tensor_scalar(ap(o), ap(a), val(s1), None, f1), views(a, s1), [o])
+        return op("v", lambda: g.vector.tensor_scalar(ap(o), ap(a), val(s1), val(s2), f1, f2), views(a, s1, s2), [o])
+
+    def scan(o, a, b, init, f0, f1):
+        return op("v", lambda: g.vector.tensor_tensor_scan(ap(o), ap(a), ap(b), init, f0, f1), [a, b], [o])
+
+    def tr(o, i):
+        return op("v", lambda: g.vector.transpose(ap(o), ap(i)), [i], [o])
+
+    def red(o, i):
+        return op("v", lambda: g.vector.tensor_reduce(ap(o), ap(i), AxisListType.X, A.max), [i], [o])
+
+    def act(o, i, f=AF.Identity, bias=None, scale=None, acc=None, ind=None):
+        kw = {}
+        if bias is not None:
+            kw["bias"] = val(bias)
+        if scale is not None:
+            kw["scale"] = scale
+        if acc is not None:
+            kw["accum_out"] = ap(acc)
+        return op("a", lambda: g.scalar.activation(ap(o), src(i, ind), f, **kw), views(i, bias, ind), views(o, acc))
+
+    def fill(o, c):
+        return act(o, W("ones", 0, len(cols(o))), scale=float(c))
+
+    def quant(q, s, i):
+        return op("v", lambda: g.vector.quantize_mx(ap(q), ap(s), ap(i)), [i], [q, s])
+
+    def mx(o, lq_, ls_, rq, rs_):
+        return op("t", lambda: g.tensor.matmul_mx(ap(o), ap(lq_), ap(ls_), ap(rq), ap(rs_), True, True), [lq_, ls_, rq, rs_], [o])
+
+    def pickq(o, i, ind):
+        return op("v", lambda: g.vector.tensor_copy(ap(o).bitcast(dt.uint32), ap(i).bitcast(dt.uint32).indirect(ap(ind))), [i, ind], [o])
+
+    def picks(o, i, ind):
+        return act(o, i, AF.Copy, ind=ind)
+
+    def remote(peer, o, i, sem, mask, codes=False):
+        order("g", [i], [])
+        rid, pid = topo.addr(peer)[0], topo.addr(peer)[1]
+        oa, ia = ap(o), ap(i)
+        if codes:
+            oa, ia = oa.bitcast(dt.uint8), ia.bitcast(dt.uint8)
+        g.remote_dma(oa, ia, T.sem[sem], T.sem["sent"], pid, rid, mask)
+        count["sent"] = count.get("sent", 0) + bin(mask).count("1")
+
+    def col(name, c):
+        return W(name, c, c + 1)
+
+    def blk(name, b):
+        return W(name, 128 * b, 128 * b + 128)
+
+    hx = V + HC
+    dma("a", T.ut[:], T.u[:], [], [W("ut")])
+    dma("s", T.x0[:, 4 * V:4 * hx], T.x[:, 0:4 * HC], [], [W("x0", 4 * V, 4 * hx)])
+    dma("a", T.x0[:, 0:4 * V], T.x[:, 4 * (C - V):4 * C], [], [W("x0", 0, 4 * V)])
+    ex0 = dma("s", T.x0[:, 4 * hx:4 * (V + C)], T.x[:, 4 * HC:4 * C], [], [W("x0", 4 * hx, 4 * (V + C))])
+    dma("a", T.x0[:, 4 * (V + C):4 * CE], T.x[:, 0:4 * V], [], [W("x0", 4 * (V + C), 4 * CE)])
+    need("s", ex0)
+    dma("s", T.qw[:].bitcast(dt.uint8), T.wc[:], [], [W("qw")])
+    dma("s", T.sw[:], T.ws[:], [], [W("sw")])
+    dma("s", T.vt[:], T.v[:], [], [W("vt")])
+
+    pnum = col("pj", 7)
+    op("g", lambda: g.iota(ap(pnum), [[1, 1]], 0, 1), [], [pnum])
+    op("g", lambda: g.iota(ap(W("rp")), [[1, 64]], 0, 0, allow_small_or_imprecise_dtypes=True), [], [W("rp")])
+    op("g", lambda: g.iota(ap(W("r16")), [[0, NT], [1, 16]], 0, 0, allow_small_or_imprecise_dtypes=True), [], [W("r16")])
+    op("v", lambda: g.vector.memset(ap(W("ones")), 1.0), [], [W("ones")])
+    op("g", lambda: g.affine_select(ap(W("eb")), ap(W("ones")), [[1, 528]], A.is_equal, 0.0, -3, -4), [W("ones")], [W("eb")])
+    for k, m in enumerate((15, 31, 16)):
+        ts(col("pj", k), pnum, m, A.bitwise_and)
+    ts(col("pj", 5), pnum, 15, A.add)
+    ts(col("pj", 6), pnum, 1, A.add)
+    ts(W("lu"), W("rp", 0, 8), 16.0, A.mult)
+    ts(W("pj", 3, 5), W("pj", 5, 7), 15, A.bitwise_and)
+    cp(W("pf", 0, 5), W("pj", 0, 5))
+    icol, p32, e16, im1, ip1 = (col("pf", k) for k in range(5))
+    ts(col("cl", 0), icol, float(NT), A.mult, float(V), A.add)
+    ts(W("nn"), W("rp", 0, 32), 16.0, A.mult, icol, A.add)
+    ts(W("lpi"), W("rp", 0, NT), col("cl", 0), A.add)
+    ts(W("lrot", 0, 2), W("rp", 0, 2), 16.0, A.mult, im1, A.add)
+    ts(W("lrot", 2, 4), W("rp", 0, 2), 16.0, A.mult, ip1, A.add)
+    ts(W("mk"), W("r16"), icol, A.is_equal)
+    n4, n24 = W("nn", 0, 4), W("nn", 0, 24)
+    for n in ("ao0", "ap0"):
+        fill(W(n, NT, 32), 0.0)
+    fill(W("rs"), 0.0)
+    fill(W("kp"), 1.0)
+    act(W("k4", 0, 4), n4, AF.Sign, bias=0.5 - V)
+    act(W("k4", 4, 8), n4, AF.Sign, bias=0.5 - V - NT)
+    act(W("k4", 8, 12), W("k4", 0, 4), bias=30.0, scale=-26.0)
+    act(W("k4", 12, 16), W("k4", 4, 8), scale=22.0)
+    act(W("nm"), W("mk"), bias=1.0, scale=-1.0)
+    tt(W("k4", 16, 20), W("k4", 8, 12), W("k4", 12, 16), A.add)
+    tt(W("k4", 20, 24), W("k4", 16, 20), n4, A.add)
+    cp(W("lc1"), W("k4", 20, 24))
+
+    def list_terms():
+        act(W("k4", 24, 28), n4, bias=-908.0, scale=18.0)
+        act(W("k4", 28, 32), n4, bias=1182.0)
+        act(W("k4", 32, 36), W("k4", 4, 8), scale=-4.0)
+        act(W("k6", 0, 4), n4, AF.Abs, bias=0.5 - NT)
+        act(W("k6", 4, 8), n4, AF.Sign, bias=0.5 - NT)
+        act(W("k3", 0, 24), n24, AF.Sign, bias=0.5 - V)
+        act(W("k3", 24, 48), n24, AF.Sign, bias=0.5 - V - C)
+        act(W("k6", 8, 12), W("k6", 4, 8), bias=1.5 * NT - 0.5, scale=NT / 2)
+        act(W("k3", 48, 72), W("k3", 0, 24), bias=-16.0 * V, scale=-8.0 * C)
+        act(W("k3", 72, 96), W("k3", 24, 48), scale=-8.0 * C)
+        act(W("k3", 96, 120), n24, scale=16.0)
+        act(W("k2", 24, 44), W("nn", 0, NT), scale=16.0)
+        fill(W("rs", 0, HK, KW), BIG)
+        fill(W("kp", 0, HK, KW), 0.0)
+
+    def scalar_constants():
+        fill(W("cs", 2 * HK, 1184), 0.0)
+        fill(W("kk"), 1.0)
+        fill(W("ex"), 1.0)
+        act(W("r65"), W("rp"), scale=65.0)
+        act(W("cb"), W("rp", 0, 32), bias=2.0 * V / 64, scale=65.0 / 64)
+        fill(col("kk", NT), 0.0)
+        act(col("cl", 1), icol, bias=64.0 * 401 + 2 * V, scale=64.0 * NT)
+        act(col("cl", 2), icol, bias=64.0 * (400 + C - 2 * NT + 1) + 2 * V, scale=-64.0 * NT)
+        act(col("cl", 3), icol, bias=2.0 * V, scale=float(NT))
+        act(col("cl", 4), e16, bias=-8.0, scale=-0.5)
+        act(col("cl", 5), e16, bias=0.5, scale=-0.5)
+        act(col("cl", 6), e16, bias=-7.5, scale=-1.0)
+        act(col("cl", 7), icol, bias=-7.25e6, scale=0.5e6)
+        act(col("cl", 8), icol, bias=0.25e6, scale=-0.5e6)
+        act(W("ckb", 0, NT), W("rp", 0, NT), bias=col("cl", 1), scale=64.0)
+        act(W("ckb", NT, 48), W("rp", NT, 48), bias=col("cl", 2), scale=64.0)
+        act(W("cc", 0, NT), W("rp", 0, NT), bias=col("cl", 3))
+        act(W("cc", NT, 48), W("rp", 0, 48 - NT), bias=col("cl", 3))
+        act(col("cl", 9), p32, bias=col("cl", 4), scale=-0.5)
+        act(col("cl", 10), p32, bias=col("cl", 5), scale=-0.5)
+        r32 = W("rp", 0, 32)
+        act(W("k7", 64, 96), r32, AF.Abs, bias=col("cl", 6))
+        act(W("k7", 0, 32), r32, AF.Abs, bias=col("cl", 9))
+        act(W("k7", 32, 64), r32, AF.Abs, bias=col("cl", 10))
+        act(W("k7", 96, 128), W("k7", 64, 96), AF.Relu, bias=-8.0e6, scale=1.0e6)
+        act(W("cz", 0, 32), W("k7", 0, 32), AF.Relu, bias=col("cl", 7), scale=1.0e6)
+        act(W("cz", 64, 96), W("k7", 32, 64), AF.Relu, bias=col("cl", 8), scale=1.0e6)
+        act(W("cz", 32, 64), W("k7", 96, 128), bias=64.0 * 400)
+        act(W("cz", 96, 128), W("k7", 96, 128), bias=64.0 * 400)
+
+    def vector_constants():
+        tt(W("k4", 36, 40), W("k4", 0, 4), W("k4", 4, 8), A.subtract)
+        tt(W("k4", 40, 44), W("k4", 28, 32), W("k4", 32, 36), A.add)
+        tt(W("k1", 0, 24), W("k3", 48, 72), W("k3", 72, 96), A.add)
+        tt(W("k4", 44, 48), W("k4", 36, 40), W("k4", 24, 28), A.mult)
+        ts(W("ldup"), W("k6", 0, 4), -1.0, A.mult, NT - 0.5, A.add)
+        tt(W("k2", 0, 24), W("k1", 0, 24), W("k3", 96, 120), A.add)
+        tt(W("k4", 48, 52), W("k4", 44, 48), W("k4", 40, 44), A.add)
+        tt(W("k6", 12, 16), W("k6", 8, 12), W("k6", 0, 4), A.subtract)
+        ts(W("k5", 0, 44), W("k2", 0, 44), -8.0 * (NT - 1), A.add, 1.0 / C, A.mult)
+        cp(W("lc2"), W("k4", 48, 52))
+        cp(W("lfin"), W("k6", 12, 16))
+        ts(W("k1", 0, 44), W("k5", 0, 44), -float(C - 1), A.mult)
+        for b in range(4):
+            quant(blk("qe", b), blk("se", b), W("eb", 3 - b, 515 - b))
+        tt(W("k9", 0, 44), W("k1", 0, 44), W("k2", 0, 44), A.add)
+        cp(W("lnr"), W("k9", 0, 24))
+        cp(W("lnf"), W("k9", 24, 44))
+
+    def neighbours(buf, stride, base, t1, t2):
+        tr(W(t1), W(buf, stride - 1, 32 * stride, stride))
+        cp(W(t2), W(t1), W("lrot"))
+        tr(W(buf, base, base + 64), W(t2))
+
+    used = topo.mask(core, T.cores[rank ^ STEP[0]])
+
+    def masks(r):
+        full = topo.mask(core, T.cores[rank ^ STEP[r]])
+        return full, full & used
+
+    def scores(r, h):
+        a, b = HC * h, HC * h + HC
+        mx(W("pb%d" % h, 0, HC), W("qur"), W("sur"), W("qp%d" % r, a, b), W("sp%d" % r, a, b))
+
+    def own_scores(r, h):
+        a, b = HC * h, HC * h + HC
+        tt(W("sm", a, b), W("pb%d" % h, 0, HC), W("mk", a, b), A.mult)
+        scan(W("sc", a, b), W("nm", a, b), W("sm", a, b), 0.0, A.mult, A.add)
+
+    def send_scores(r, t0, t1, sem):
+        cp(W("ao%d" % r, t0, t1), W("sc", 16 * t0 + 15, 16 * t1, 16))
+        note(None, sem, bin(masks(r)[1]).count("1"), [], [W("ap%d" % r, t0, t1)])
+        remote(T.cores[rank ^ STEP[r]], W("ap%d" % r, t0, t1), W("ao%d" % r, t0, t1), sem, masks(r)[1])
+
+    quant(W("qu"), W("su"), W("ut"))
+    pickq(W("qur"), W("qu"), W("lu"))
+    picks(W("sur"), W("su"), W("lu"))
+    list_terms()
+    quant(W("qn0", 0, hx), W("sn0", 0, hx), W("x0", 0, 4 * hx))
+    remote(T.cores[rank ^ STEP[0]], W("ls0", 0, hx), W("sn0", 0, hx), "ab0", used)
+    quant(W("qn0", hx, CE), W("sn0", hx, CE), W("x0", 4 * hx, 4 * CE))
+    for h in range(2):
+        picks(W("sp0", HC * h, HC * h + HC), W("sn0", 0, CE), W("lpi", HT * h, HT * h + HT))
+        pickq(W("qp0", HC * h, HC * h + HC), W("qn0", 0, CE), W("lpi", HT * h, HT * h + HT))
+        scores(0, h)
+    scalar_constants()
+    own_scores(0, 0)
+    own_scores(0, 1)
+    send_scores(0, 0, NT, "aw0")
+
+    for r in range(R):
+        peer = T.cores[rank ^ STEP[r]]
+        full = masks(r)[0]
+        qp, sp, qn, sn = "qp%d" % r, "sp%d" % r, "qn%d" % r, "sn%d" % r
+        wo, wp, lq, ls, ao, pa = "wo%d" % r, "wp%d" % r, "lq%d" % r, "ls%d" % r, "ao%d" % r, "ap%d" % r
+        note(None, "ab%d" % r, (2 if r else 3) * bin(full).count("1"), [], [W(lq), W(ls)])
+        if r > 0:
+            picks(W(sn), W(sp), W("lnr", 0, PW // 16))
+        neighbours(ao, 1, 32, "t1", "t2")
+        cp(W(wo), W(ao), W("lc1"))
+        if r > 0:
+            pickq(W(qn), W(qp), W("lnr", 0, PW // 16))
+        remote(peer, W(lq), W(qn, 0, CE), "ab%d" % r, full, True)
+        s0 = 0 if r else hx
+        remote(peer, W(ls, s0, CE), W(sn, s0, CE), "ab%d" % r, full)
+        if r == 0:
+            vector_constants()
+        for b in range(4):
+            mx(W("pb%d" % (4 + b), 0, C), blk("qe", b), blk("se", b), W(qp), W(sp))
+        for b in range(4):
+            mx(W("pb%d" % b, 0, CE), blk("qe", b), blk("se", b), W(lq), W(ls))
+
+        def seg(name, s):
+            return W(name, KW * s, KW * s + KW)
+
+        def half(name, k):
+            return W(name, HK * k, HK * k + HK)
+
+        def least(k):
+            scan(half("mm", k), W("rs"), half("dd", k), 0.0, A.max, A.min)
+
+        def above(k):
+            for t in range(HT * k, HT * k + HT):
+                ts(seg("fl", t), seg("mm", t), col("mm", KW * t + KW - 1), A.is_gt)
+
+        def tally(k):
+            scan(half("cs", k), W("kp"), half("fl", k), 0.0, A.mult, A.add)
+
+        def signs(k):
+            for t in range(HT * k, HT * k + HT):
+                s = seg("mm", NT + t)
+                act(seg("jk", t), s, AF.Sign, bias=col("mm", s[2] - 1), scale=-1.0, acc=col("nd", t))
+
+        for t in range(NT):
+            act(seg("dd", t), W(wo, t, t + KW), AF.Abs, bias=col(pa, t), scale=-1.0)
+        if r > 0:
+            least(0)
+        neighbours(pa, 1, 32, "t1", "t2")
+        cp(W(wp), W(pa), W("lc1"))
+        for t in range(NT):
+            act(seg("dd", NT + t), W(wp, t, t + KW), AF.Abs, bias=col(ao, t), scale=-1.0)
+        if r == 0:
+            least(0)
+        above(0)
+        least(1)
+        least(2)
+        signs(0)
+        tally(0)
+        least(3)
+        signs(1)
+        above(1)
+        tally(1)
+        neighbours("cs", KW, 1184, "t1b", "t2b")
+        tt(W("bi", 0, HT), W("nd", 0, HT), W("cb", 0, HT), A.subtract)
+        tt(W("cd"), W("cs"), W("r65"), A.add, W("lc2"))
+        nka = NT - NKD
+
+        def back(t):
+            act(seg("jk", t), W("cd", t, t + KW), AF.Sign, bias=col("bi", t), scale=1.0 / 64, acc=col("ks", KW * t + KW - 1))
+
+        for t in range(min(nka, HT)):
+            back(t)
+        tt(W("bi", HT, NT), W("nd", HT, NT), W("cb", HT, NT), A.subtract)
+        for t in range(HT, nka):
+            back(t)
+        act(W("ex", 0, nka), W("nd", 0, nka), bias=2.0 * V, scale=2.0)
+        tt(W("kb"), W("nd", 0, NT), W("ckb"), A.add, W("ldup", 0, 3))
+        for t in range(nka, NT):
+            ts(seg("f2", t - nka), W("cd", t, t + KW), -1.0 / 64, A.mult, col("bi", t), A.is_equal)
+        scan(W("ks", KW * nka, 2 * HK), W("kp", 0, KW * NKD), W("f2", 0, KW * NKD), 0.0, A.mult, A.add)
+        for b in range(4):
+            act(W("psb", PW * b, PW * b + CE), W("pb%d" % b, 0, CE), scale=0.5)
+        tt(W("ok", 0, NT), W("ks", KW - 1, 2 * HK, KW), W("ex", 0, NT), A.is_equal)
+        tt(W("ky"), W("ok", 0, NT), W("kb"), A.mult, W("ldup", 0, 3))
+        scan(W("lo"), W("kk"), W("ky"), 0.0, A.mult, A.max)
+        ts(W("zz", 0, 32), W("cz", 0, 32), -1.0, A.mult, col("lo", NT - 1), A.add)
+        ts(W("zz", 32, 96), W("cz", 32, 96), -1.0, A.mult, col("lo", 2 * NT - 1), A.add)
+        ts(W("zz", 96, 128), W("cz", 96, 128), -1.0, A.mult, col("lo", NT - 1), A.add)
+        tr(W("zt"), W("zz"))
+        red(col("cl", 12), W("zt", 0, 64))
+        red(col("cl", 13), W("zt", 64, 128))
+        ts(W("fi", 0, NT), W("lo", 0, NT), col("cl", 12), A.max, float(V), A.max)
+        ts(W("fi", NT, 2 * NT), W("lo", NT, 2 * NT), col("cl", 13), A.max, float(V), A.max)
+        ts(W("lw", 0, 2 * NT), W("fi", 0, 2 * NT), 63, A.bitwise_and)
+        tt(W("na"), W("lw", 0, 2 * NT), W("cc", 0, 48), A.subtract, W("lfin", 0, 3))
+        ts(W("off", 0, 2 * NT), W("na", 0, 2 * NT), -1.0, A.mult)
+        nq, ns = "qp%d" % (r + 1), "sp%d" % (r + 1)
+
+        def plane(b):
+            return W("psb", PW * b, PW * b + CE)
+
+        def part(name, b, h):
+            return W(name, C * b + HC * h, C * b + HC * h + HC)
+
+        for h in range(2):
+            for b in range(4):
+                hoff = W("off", NT + HT * h, NT + HT * h + HT)
+                if (h, b) == (0, 1):
+                    cp(part("hb", b, h), plane(b), hoff)
+                else:
+                    act(part("hb", b, h), plane(b), AF.Copy, ind=hoff)
+        for h in range(2):
+            a = HC * h
+            for b in range(4):
+                tt(W("yt", 4 * a + b, 4 * (a + HC), 4), plane(b), part("hb", b, h), A.add, W("off", HT * h, HT * h + HT))
+            quant(W("qy", a, a + HC), W("sy", a, a + HC), W("yt", 4 * a, 4 * (a + HC)))
+            for b in range(4):
+                mx(W("pb%d" % b, 0, HC), blk("qw", b), blk("sw", b), W("qy", a, a + HC), W("sy", a, a + HC))
+                act(part("rl", b, h), W("pb%d" % b, 0, HC), AF.Relu, scale=0.03125)
+        if r == 0:
+            for k in range(1, R):
+                fill(W("ao%d" % k, NT, 32), 0.0)
+                fill(W("ap%d" % k, NT, 32), 0.0)
+            act(W("cc", 48, 96), W("cc", 0, 48), bias=float(V), scale=-1.0)
+
+        def state(h, b0, b1):
+            for b in range(b0, b1):
+                tt(W("xt", 4 * HC * h + b, 4 * HC * (h + 1), 4), part("rl", b, h), W("pb%d" % (4 + b), HC * h, HC * h + HC), A.add)
+
+        def pack(h):
+            quant(W(nq, HC * h, HC * h + HC), W(ns, HC * h, HC * h + HC), W("xt", 4 * HC * h, 4 * HC * (h + 1)))
+
+        state(0, 0, 4)
+        pack(0)
+        if r < R - 1:
+            scores(r + 1, 0)
+            state(1, 0, 1)
+            own_scores(r + 1, 0)
+            send_scores(r + 1, 0, HT, "aw%d" % (r + 1))
+            state(1, 1, 4)
+            pack(1)
+            scores(r + 1, 1)
+            if r == 0:
+                quant(W("qv"), W("sv"), W("vt"))
+            own_scores(r + 1, 1)
+            send_scores(r + 1, HT, NT, "ax%d" % (r + 1))
+        else:
+            state(1, 0, 4)
+            pack(1)
+
+    qp, sp, qn, sn = "qp%d" % R, "sp%d" % R, "qn%d" % R, "sn%d" % R
+    for h in range(2):
+        a, b = HC * h, HC * h + HC
+        picks(W(sn, a, b), W(sp), W("lnf", HT * h, HT * h + HT))
+        pickq(W(qn, a, b), W(qp), W("lnf", HT * h, HT * h + HT))
+        mx(W("pb%d" % h, 0, HC), W("qv"), W("sv"), W(qn, a, b), W(sn, a, b))
+    tt(W("odt"), W("cc", 48, 96), W("na"), A.subtract)
+    dma("s", T.oc[:, 0:4 * HC], T[qn][:, 0:HC].bitcast(dt.uint8), [W(qn, 0, HC)], [])
+    act(W("yo", 0, HC), W("pb0", 0, HC))
+    dma("a", T.y[:, 0:HC], T.yo[:, 0:HC], [W("yo", 0, HC)], [])
+    dma("s", T.oc[:, 4 * HC:4 * C], T[qn][:, HC:C].bitcast(dt.uint8), [W(qn, HC, C)], [])
+    cp(W("yo", HC, C), W("pb1", 0, HC))
+    for k in range(4):
+        dma("a", T.osc[4 * k:4 * k + 4, :], T[sn][32 * k:32 * k + 4, 0:C], [W(sn, 0, C)], [])
+    dma("s", T.y[:, HC:C], T.yo[:, HC:C], [W("yo", HC, C)], [])
+    dma("s", T.od[:, 0:C], T.odt[:, 0:NT], [W("odt")], [])
+    dma("s", T.od[:, C:2 * C], T.odt[:, NT:2 * NT], [W("odt")], [])
+    last = {events[e][0]: e for e in range(len(events))}
+    for sem in sorted(count, key=lambda s: last.get(s, 0)):
+        if all(known[q].get(sem, 0) < count[sem] for q in known):
+            g.wait_ge(T.sem[sem], count[sem])

@@ -9,7 +9,8 @@ HK = HT * KW
 HC = C // 2
 CE = C + 2 * V
 PW = 368
-NKD = 9
+NKD = 8
+PICK = [(0, 8), (8, 16), (16, 23)]
 BIG = 1.0e29
 F32, BF, I32, U16, Q4, U8 = "float32", "bfloat16", "int32", "uint16", "float8_e4m3fn_x4", "uint8"
 
@@ -310,16 +311,19 @@ def rank_program(g, core, T, topo):
         cp(W("lc2"), W("k4", 48, 52))
         cp(W("lfin"), W("k6", 12, 16))
         ts(W("k1", 0, 44), W("k5", 0, 44), -float(C - 1), A.mult)
-        for b in range(4):
-            quant(blk("qe", b), blk("se", b), W("eb", 3 - b, 515 - b))
         tt(W("k9", 0, 44), W("k1", 0, 44), W("k2", 0, 44), A.add)
         cp(W("lnr"), W("k9", 0, 24))
         cp(W("lnf"), W("k9", 24, 44))
 
     def neighbours(buf, stride, base, t1, t2):
-        tr(W(t1), W(buf, stride - 1, 32 * stride, stride))
-        cp(W(t2), W(t1), W("lrot"))
-        tr(W(buf, base, base + 64), W(t2))
+        return [lambda: tr(W(t1), W(buf, stride - 1, 32 * stride, stride)), lambda: cp(W(t2), W(t1), W("lrot")),
+                lambda: tr(W(buf, base, base + 64), W(t2))]
+
+    def weave(chain, fillers):
+        for k, f in enumerate(chain):
+            f()
+            if k < len(fillers):
+                fillers[k]()
 
     used = topo.mask(core, T.cores[rank ^ STEP[0]])
 
@@ -331,9 +335,10 @@ def rank_program(g, core, T, topo):
         a, b = HC * h, HC * h + HC
         mx(W("pb%d" % h, 0, HC), W("qur"), W("sur"), W("qp%d" % r, a, b), W("sp%d" % r, a, b))
 
-    def own_scores(r, h):
-        a, b = HC * h, HC * h + HC
-        tt(W("sm", a, b), W("pb%d" % h, 0, HC), W("mk", a, b), A.mult)
+    def mask_scores(h):
+        tt(W("sm", HC * h, HC * h + HC), W("pb%d" % h, 0, HC), W("mk", HC * h, HC * h + HC), A.mult)
+
+    def own_scores(a, b):
         scan(W("sc", a, b), W("nm", a, b), W("sm", a, b), 0.0, A.mult, A.add)
 
     def send_scores(r, t0, t1, sem):
@@ -353,8 +358,10 @@ def rank_program(g, core, T, topo):
         pickq(W("qp0", HC * h, HC * h + HC), W("qn0", 0, CE), W("lpi", HT * h, HT * h + HT))
         scores(0, h)
     scalar_constants()
-    own_scores(0, 0)
-    own_scores(0, 1)
+    mask_scores(0)
+    own_scores(0, HC)
+    mask_scores(1)
+    own_scores(HC, C)
     send_scores(0, 0, NT, "aw0")
 
     for r in range(R):
@@ -363,12 +370,13 @@ def rank_program(g, core, T, topo):
         qp, sp, qn, sn = "qp%d" % r, "sp%d" % r, "qn%d" % r, "sn%d" % r
         wo, wp, lq, ls, ao, pa = "wo%d" % r, "wp%d" % r, "lq%d" % r, "ls%d" % r, "ao%d" % r, "ap%d" % r
         note(None, "ab%d" % r, (2 if r else 3) * bin(full).count("1"), [], [W(lq), W(ls)])
+        chain = neighbours(ao, 1, 32, "t1", "t2") + [lambda: cp(W(wo), W(ao), W("lc1"))]
         if r > 0:
-            picks(W(sn), W(sp), W("lnr", 0, PW // 16))
-        neighbours(ao, 1, 32, "t1", "t2")
-        cp(W(wo), W(ao), W("lc1"))
-        if r > 0:
-            pickq(W(qn), W(qp), W("lnr", 0, PW // 16))
+            for a, b in PICK:
+                picks(W(sn, 16 * a, 16 * b), W(sp), W("lnr", a, b))
+            weave(chain, [lambda a=a, b=b: pickq(W(qn, 16 * a, 16 * b), W(qp), W("lnr", a, b)) for a, b in PICK])
+        else:
+            weave(chain, [lambda b=b: quant(blk("qe", b), blk("se", b), W("eb", 3 - b, 515 - b)) for b in range(4)])
         remote(peer, W(lq), W(qn, 0, CE), "ab%d" % r, full, True)
         s0 = 0 if r else hx
         remote(peer, W(ls, s0, CE), W(sn, s0, CE), "ab%d" % r, full)
@@ -385,12 +393,12 @@ def rank_program(g, core, T, topo):
         def half(name, k):
             return W(name, HK * k, HK * k + HK)
 
-        def least(k):
-            scan(half("mm", k), W("rs"), half("dd", k), 0.0, A.max, A.min)
+        def least(k, t0=0, t1=HT):
+            a, b = HK * k + KW * t0, HK * k + KW * t1
+            scan(W("mm", a, b), W("rs", 0, b - a), W("dd", a, b), 0.0, A.max, A.min)
 
-        def above(k):
-            for t in range(HT * k, HT * k + HT):
-                ts(seg("fl", t), seg("mm", t), col("mm", KW * t + KW - 1), A.is_gt)
+        def above(t):
+            ts(seg("fl", t), seg("mm", t), col("mm", KW * t + KW - 1), A.is_gt)
 
         def tally(k):
             scan(half("cs", k), W("kp"), half("fl", k), 0.0, A.mult, A.add)
@@ -402,40 +410,49 @@ def rank_program(g, core, T, topo):
 
         for t in range(NT):
             act(seg("dd", t), W(wo, t, t + KW), AF.Abs, bias=col(pa, t), scale=-1.0)
+        chain = neighbours(pa, 1, 32, "t1", "t2") + [lambda: cp(W(wp), W(pa), W("lc1"))]
         if r > 0:
-            least(0)
-        neighbours(pa, 1, 32, "t1", "t2")
-        cp(W(wp), W(pa), W("lc1"))
+            least(0, 0, 5)
+            least(0, 5, HT)
+            weave(chain, [lambda t=t: above(t) for t in range(3)])
+        else:
+            weave(chain, [])
         for t in range(NT):
             act(seg("dd", NT + t), W(wp, t, t + KW), AF.Abs, bias=col(ao, t), scale=-1.0)
         if r == 0:
             least(0)
-        above(0)
+        for t in range(3 if r else 0, HT):
+            above(t)
         least(1)
+        if r > 0:
+            tally(0)
         least(2)
         signs(0)
-        tally(0)
-        least(3)
-        signs(1)
-        above(1)
+        if r == 0:
+            tally(0)
+        for t in range(HT, NT):
+            above(t)
+        least(3, 0, 5)
         tally(1)
-        neighbours("cs", KW, 1184, "t1b", "t2b")
-        tt(W("bi", 0, HT), W("nd", 0, HT), W("cb", 0, HT), A.subtract)
-        tt(W("cd"), W("cs"), W("r65"), A.add, W("lc2"))
+        least(3, 5, HT)
+        signs(1)
+        weave(neighbours("cs", KW, 1184, "t1b", "t2b") + [lambda: tt(W("cd"), W("cs"), W("r65"), A.add, W("lc2"))],
+              [lambda: tt(W("bi", 0, HT), W("nd", 0, HT), W("cb", 0, HT), A.subtract),
+               lambda: ts(W("ex", 0, HT), W("nd", 0, HT), 2.0, A.mult, 2.0 * V, A.add)])
         nka = NT - NKD
 
         def back(t):
             act(seg("jk", t), W("cd", t, t + KW), AF.Sign, bias=col("bi", t), scale=1.0 / 64, acc=col("ks", KW * t + KW - 1))
 
-        for t in range(min(nka, HT)):
+        for t in range(HT):
             back(t)
         tt(W("bi", HT, NT), W("nd", HT, NT), W("cb", HT, NT), A.subtract)
         for t in range(HT, nka):
             back(t)
-        act(W("ex", 0, nka), W("nd", 0, nka), bias=2.0 * V, scale=2.0)
         tt(W("kb"), W("nd", 0, NT), W("ckb"), A.add, W("ldup", 0, 3))
         for t in range(nka, NT):
             ts(seg("f2", t - nka), W("cd", t, t + KW), -1.0 / 64, A.mult, col("bi", t), A.is_equal)
+        ts(W("ex", HT, nka), W("nd", HT, nka), 2.0, A.mult, 2.0 * V, A.add)
         scan(W("ks", KW * nka, 2 * HK), W("kp", 0, KW * NKD), W("f2", 0, KW * NKD), 0.0, A.mult, A.add)
         for b in range(4):
             act(W("psb", PW * b, PW * b + CE), W("pb%d" % b, 0, CE), scale=0.5)
@@ -452,7 +469,8 @@ def rank_program(g, core, T, topo):
         ts(W("fi", NT, 2 * NT), W("lo", NT, 2 * NT), col("cl", 13), A.max, float(V), A.max)
         ts(W("lw", 0, 2 * NT), W("fi", 0, 2 * NT), 63, A.bitwise_and)
         tt(W("na"), W("lw", 0, 2 * NT), W("cc", 0, 48), A.subtract, W("lfin", 0, 3))
-        ts(W("off", 0, 2 * NT), W("na", 0, 2 * NT), -1.0, A.mult)
+        ts(W("off", NT, 2 * NT), W("na", NT, 2 * NT), -1.0, A.mult)
+        ts(W("off", 0, NT), W("na", 0, NT), -1.0, A.mult)
         nq, ns = "qp%d" % (r + 1), "sp%d" % (r + 1)
 
         def plane(b):
@@ -461,26 +479,16 @@ def rank_program(g, core, T, topo):
         def part(name, b, h):
             return W(name, C * b + HC * h, C * b + HC * h + HC)
 
-        for h in range(2):
-            for b in range(4):
-                hoff = W("off", NT + HT * h, NT + HT * h + HT)
-                if (h, b) == (0, 1):
-                    cp(part("hb", b, h), plane(b), hoff)
-                else:
-                    act(part("hb", b, h), plane(b), AF.Copy, ind=hoff)
-        for h in range(2):
+        def fetch(h, b):
             a = HC * h
-            for b in range(4):
-                tt(W("yt", 4 * a + b, 4 * (a + HC), 4), plane(b), part("hb", b, h), A.add, W("off", HT * h, HT * h + HT))
+            tt(W("yt", 4 * a + b, 4 * (a + HC), 4), plane(b), part("hb", b, h), A.add, W("off", HT * h, HT * h + HT))
+
+        def layer(h):
+            a = HC * h
             quant(W("qy", a, a + HC), W("sy", a, a + HC), W("yt", 4 * a, 4 * (a + HC)))
             for b in range(4):
                 mx(W("pb%d" % b, 0, HC), blk("qw", b), blk("sw", b), W("qy", a, a + HC), W("sy", a, a + HC))
                 act(part("rl", b, h), W("pb%d" % b, 0, HC), AF.Relu, scale=0.03125)
-        if r == 0:
-            for k in range(1, R):
-                fill(W("ao%d" % k, NT, 32), 0.0)
-                fill(W("ap%d" % k, NT, 32), 0.0)
-            act(W("cc", 48, 96), W("cc", 0, 48), bias=float(V), scale=-1.0)
 
         def state(h, b0, b1):
             for b in range(b0, b1):
@@ -489,41 +497,70 @@ def rank_program(g, core, T, topo):
         def pack(h):
             quant(W(nq, HC * h, HC * h + HC), W(ns, HC * h, HC * h + HC), W("xt", 4 * HC * h, 4 * HC * (h + 1)))
 
-        state(0, 0, 4)
+        for h in range(2):
+            for b in range(4):
+                hoff = W("off", NT + HT * h, NT + HT * h + HT)
+                if (h, b) == (0, 1):
+                    cp(part("hb", b, h), plane(b), hoff)
+                else:
+                    act(part("hb", b, h), plane(b), AF.Copy, ind=hoff)
+        if r == R - 1:
+            tt(W("odt"), W("cc", 48, 96), W("na"), A.subtract)
+            dma("s", T.od[:, 0:C], T.odt[:, 0:NT], [W("odt")], [])
+            dma("s", T.od[:, C:2 * C], T.odt[:, NT:2 * NT], [W("odt")], [])
+        for b in (1, 0, 2, 3):
+            fetch(0, b)
+        fetch(1, 0)
+        layer(0)
+        for b in range(1, 4):
+            fetch(1, b)
+        state(0, 0, 1)
+        layer(1)
+        if r == 0:
+            for k in range(1, R):
+                fill(W("ao%d" % k, NT, 32), 0.0)
+                fill(W("ap%d" % k, NT, 32), 0.0)
+            act(W("cc", 48, 96), W("cc", 0, 48), bias=float(V), scale=-1.0)
+        state(0, 1, 4)
+        if r == 0:
+            quant(W("qv"), W("sv"), W("vt"))
         pack(0)
         if r < R - 1:
             scores(r + 1, 0)
-            state(1, 0, 1)
-            own_scores(r + 1, 0)
+            state(1, 0, 2)
+            mask_scores(0)
+            state(1, 2, 3)
+            own_scores(0, HC)
+            state(1, 3, 4)
             send_scores(r + 1, 0, HT, "aw%d" % (r + 1))
-            state(1, 1, 4)
             pack(1)
             scores(r + 1, 1)
-            if r == 0:
-                quant(W("qv"), W("sv"), W("vt"))
-            own_scores(r + 1, 1)
+            mask_scores(1)
+            own_scores(HC, C)
             send_scores(r + 1, HT, NT, "ax%d" % (r + 1))
         else:
             state(1, 0, 4)
             pack(1)
 
     qp, sp, qn, sn = "qp%d" % R, "sp%d" % R, "qn%d" % R, "sn%d" % R
+
+    def store_scales(q, k):
+        dma(q, T.osc[4 * k:4 * k + 4, :], T[sn][32 * k:32 * k + 4, 0:C], [W(sn, 0, C)], [])
+
     for h in range(2):
         a, b = HC * h, HC * h + HC
         picks(W(sn, a, b), W(sp), W("lnf", HT * h, HT * h + HT))
         pickq(W(qn, a, b), W(qp), W("lnf", HT * h, HT * h + HT))
         mx(W("pb%d" % h, 0, HC), W("qv"), W("sv"), W(qn, a, b), W(sn, a, b))
-    tt(W("odt"), W("cc", 48, 96), W("na"), A.subtract)
     dma("s", T.oc[:, 0:4 * HC], T[qn][:, 0:HC].bitcast(dt.uint8), [W(qn, 0, HC)], [])
     act(W("yo", 0, HC), W("pb0", 0, HC))
     dma("a", T.y[:, 0:HC], T.yo[:, 0:HC], [W("yo", 0, HC)], [])
     dma("s", T.oc[:, 4 * HC:4 * C], T[qn][:, HC:C].bitcast(dt.uint8), [W(qn, HC, C)], [])
+    store_scales("s", 0)
     cp(W("yo", HC, C), W("pb1", 0, HC))
-    for k in range(4):
-        dma("a", T.osc[4 * k:4 * k + 4, :], T[sn][32 * k:32 * k + 4, 0:C], [W(sn, 0, C)], [])
+    for k in range(1, 4):
+        store_scales("a", k)
     dma("s", T.y[:, HC:C], T.yo[:, HC:C], [W("yo", HC, C)], [])
-    dma("s", T.od[:, 0:C], T.odt[:, 0:NT], [W("odt")], [])
-    dma("s", T.od[:, C:2 * C], T.odt[:, NT:2 * NT], [W("odt")], [])
     last = {events[e][0]: e for e in range(len(events))}
     for sem in sorted(count, key=lambda s: last.get(s, 0)):
         if all(known[q].get(sem, 0) < count[sem] for q in known):

@@ -5,51 +5,54 @@ STEP = [1, 2, 1]
 NT = C // 16
 KW = 2 * V + 1
 HT = NT // 2
-HK = HT * KW
+QT = NT // 4
 HC = C // 2
+CS = C + V
 CE = C + 2 * V
 PW = 368
-NKD = 8
-PICK = [(0, 8), (8, 16), (16, 23)]
+QW = 352
+NS = 10
+NA = 6
+PICK = [(0, 8), (8, 14), (14, 22)]
+SC0 = 16 * (32 - NT)
+WO, BO, BP = 96, 120, 40
 BIG = 1.0e29
+NONE, PEN, DEF = 64.0 * 1000, 64.0 * 400, 64.0 * 800 + V
 F32, BF, I32, U16, Q4, U8 = "float32", "bfloat16", "int32", "uint16", "float8_e4m3fn_x4", "uint8"
 
 _SB = {
-    "x0": (4 * CE, BF), "ut": (512, BF), "vt": (512, BF), "ones": (528, BF), "eb": (528, BF),
+    "x0": (4 * CS, BF), "ut": (512, BF), "vt": (512, BF), "ones": (528, BF), "eb": (528, BF),
     "qu": (128, Q4), "su": (128, U8), "qur": (128, Q4), "sur": (128, U8), "qv": (128, Q4), "sv": (128, U8),
     "qw": (512, Q4), "sw": (512, U8), "qe": (512, Q4), "se": (512, U8), "qy": (C, Q4), "sy": (C, U8),
     "xt": (4 * C, BF), "yt": (4 * C, BF), "hb": (4 * C, BF), "rl": (4 * C, F32), "psb": (4 * PW, BF),
-    "pj": (8, I32), "pf": (8, F32), "cl": (16, F32), "rp": (64, F32), "r16": (C, F32),
-    "mk": (C, F32), "nm": (C, F32), "sm": (C, F32), "sc": (C, F32), "t1": (32, F32), "t2": (64, F32),
-    "dd": (4 * HK, F32), "mm": (4 * HK, F32), "rs": (HK, F32), "kp": (HK, BF), "fl": (2 * HK, BF), "f2": (HK, BF),
-    "cs": (1248, BF), "t1b": (32, BF), "t2b": (64, BF), "cd": (64, F32), "r65": (64, F32),
-    "nd": (32, F32), "bi": (32, F32), "cb": (32, F32), "ex": (32, F32), "ks": (2 * HK, F32), "jk": (2 * HK, BF),
-    "ok": (32, F32), "kb": (48, F32), "ckb": (48, F32), "ky": (48, F32), "kk": (48, F32), "lo": (48, F32),
+    "pj": (8, I32), "pf": (8, F32), "cl": (16, F32), "rp": (64, F32), "r16": (C, F32), "r80": (80, F32),
+    "mk": (C, F32), "nm": (C, F32), "sm": (C, F32), "sc": (SC0 + 512, F32), "t1": (64, F32), "t2": (64, F32),
+    "t3": (32, F32), "t4": (64, F32),
+    "dd": (NT * KW, F32), "mm": (NT * KW, F32), "rs": (QT * KW, F32), "kp": (HT * KW, BF), "fl": (NT * KW, BF),
+    "f2": (NT * KW, BF), "cs": (NT * KW, BF), "cd": (64, F32), "cdc": (80, F32),
+    "nd": (32, F32), "cb": (32, F32), "ks": (NT * KW, F32), "jk": (NT * KW, BF),
+    "no": (32, F32), "kb": (48, F32), "ckb": (48, F32), "lo": (48, F32),
     "zz": (128, F32), "cz": (128, F32), "zt": (128, F32), "fi": (48, I32), "lw": (48, I32),
-    "cc": (96, F32), "na": (48, F32), "off": (48, U16), "odt": (48, F32), "yo": (C, F32),
-    "lpi": (20, U16), "lu": (8, U16), "lrot": (4, U16), "lc1": (4, U16), "lc2": (4, U16), "lnr": (24, U16),
-    "lnf": (20, U16), "ldup": (4, U16), "lfin": (4, U16),
-    "k1": (64, F32), "k2": (64, F32), "k3": (128, F32), "k4": (64, F32), "k5": (64, I32), "k6": (64, F32),
+    "cc": (48, F32), "na": (48, F32), "off": (48, U16), "odt": (48, F32), "yo": (C, F32),
+    "lpi": (20, U16), "lu": (8, U16), "lrot": (8, U16), "lc": (4, U16), "lnr": (24, U16), "lnf": (20, U16),
+    "k1": (64, F32), "k2": (64, F32), "k3": (128, F32), "k4": (64, F32), "k5": (64, I32),
     "k7": (128, F32), "k9": (64, F32), "nn": (32, F32),
+    "wo": (R * WO, F32), "ap": (R * NT, F32), "bo": (R * BO, F32), "bp": (R * BP, F32),
 }
 for _r in range(R + 1):
-    _SB["qn%d" % _r] = (PW, Q4)
-    _SB["sn%d" % _r] = (PW, U8)
+    _SB["qn%d" % _r] = (QW, Q4)
+    _SB["sn%d" % _r] = (QW, U8)
     _SB["qp%d" % _r] = (C, Q4)
     _SB["sp%d" % _r] = (C, U8)
 for _r in range(R):
-    _SB["lq%d" % _r] = (CE, Q4)
-    _SB["ls%d" % _r] = (CE, U8)
-    _SB["ao%d" % _r] = (96, F32)
-    _SB["ap%d" % _r] = (96, F32)
-    _SB["wo%d" % _r] = (64, F32)
-    _SB["wp%d" % _r] = (64, F32)
+    _SB["lq%d" % _r] = (CS, Q4)
+    _SB["ls%d" % _r] = (CS, U8)
 SCRATCH = {k: ("sbuf", [128, n], d) for k, (n, d) in _SB.items()}
 for _b in range(8):
     SCRATCH["pb%d" % _b] = ("psum", [128, 512], F32)
 NDMA = 20
 SEMAPHORES = (["cv", "ca", "ct", "cg", "sent"] + ["dm%d" % k for k in range(NDMA)]
-              + ["%s%d" % (n, k) for k in range(R) for n in ("aw", "ax", "ab")])
+              + ["%s%d" % (n, k) for k in range(R) for n in ("aw", "ax", "ay", "az", "ab")])
 
 A = AluOpType
 AF = ActivationFunctionType
@@ -75,8 +78,13 @@ def rank_program(g, core, T, topo):
     def W(name, a=0, b=None, s=1):
         return (name, a, SCRATCH[name][1][1] if b is None else b, s)
 
+    def back_to_front(v):
+        return (v[0], v[2] - 1, v[1] - 1, -1)
+
     def ap(v):
-        return T[v[0]][:, v[1]:v[2]] if v[3] == 1 else T[v[0]][:, v[1]:v[2]:v[3]]
+        if v[3] == 1:
+            return T[v[0]][:, v[1]:v[2]]
+        return T[v[0]][:, v[1]:(v[2] if v[2] >= 0 else None):v[3]]
 
     def need(q, e):
         sem, val_, clk = events[e][0], events[e][1], events[e][2]
@@ -164,7 +172,7 @@ def rank_program(g, core, T, topo):
         return op("v", lambda: g.vector.transpose(ap(o), ap(i)), [i], [o])
 
     def red(o, i):
-        return op("v", lambda: g.vector.tensor_reduce(ap(o), ap(i), AxisListType.X, A.max), [i], [o])
+        return op("v", lambda: g.vector.tensor_reduce(ap(o), ap(i), AxisListType.X, A.min), [i], [o])
 
     def act(o, i, f=AF.Identity, bias=None, scale=None, acc=None, ind=None):
         kw = {}
@@ -191,6 +199,11 @@ def rank_program(g, core, T, topo):
     def picks(o, i, ind):
         return act(o, i, AF.Copy, ind=ind)
 
+    def iota(o, pattern, mult=0):
+        if SCRATCH[o[0]][2] == I32:
+            return op("g", lambda: g.iota(ap(o), pattern, 0, mult), [], [o])
+        return op("g", lambda: g.iota(ap(o), pattern, 0, mult, allow_small_or_imprecise_dtypes=True), [], [o])
+
     def remote(peer, o, i, sem, mask, codes=False):
         order("g", [i], [])
         rid, pid = topo.addr(peer)[0], topo.addr(peer)[1]
@@ -206,22 +219,34 @@ def rank_program(g, core, T, topo):
     def blk(name, b):
         return W(name, 128 * b, 128 * b + 128)
 
+    def peer_of(r):
+        return T.cores[rank ^ STEP[r]]
+
+    short = topo.mask(core, peer_of(0))
+
+    def wide(r):
+        return (topo.mask(core, peer_of(r)) & ~short) or short
+
+    def swap(r, sem, land, out):
+        note(None, "%s%d" % (sem, r), bin(short).count("1"), [], [land])
+        remote(peer_of(r), land, out, "%s%d" % (sem, r), short)
+
     hx = V + HC
     dma("a", T.ut[:], T.u[:], [], [W("ut")])
     dma("s", T.x0[:, 4 * V:4 * hx], T.x[:, 0:4 * HC], [], [W("x0", 4 * V, 4 * hx)])
     dma("a", T.x0[:, 0:4 * V], T.x[:, 4 * (C - V):4 * C], [], [W("x0", 0, 4 * V)])
-    ex0 = dma("s", T.x0[:, 4 * hx:4 * (V + C)], T.x[:, 4 * HC:4 * C], [], [W("x0", 4 * hx, 4 * (V + C))])
-    dma("a", T.x0[:, 4 * (V + C):4 * CE], T.x[:, 0:4 * V], [], [W("x0", 4 * (V + C), 4 * CE)])
+    ex0 = dma("s", T.x0[:, 4 * hx:4 * CS], T.x[:, 4 * HC:4 * C], [], [W("x0", 4 * hx, 4 * CS)])
     need("s", ex0)
     dma("s", T.qw[:].bitcast(dt.uint8), T.wc[:], [], [W("qw")])
     dma("s", T.sw[:], T.ws[:], [], [W("sw")])
     dma("s", T.vt[:], T.v[:], [], [W("vt")])
 
     pnum = col("pj", 7)
-    op("g", lambda: g.iota(ap(pnum), [[1, 1]], 0, 1), [], [pnum])
-    op("g", lambda: g.iota(ap(W("rp")), [[1, 64]], 0, 0, allow_small_or_imprecise_dtypes=True), [], [W("rp")])
-    op("g", lambda: g.iota(ap(W("r16")), [[0, NT], [1, 16]], 0, 0, allow_small_or_imprecise_dtypes=True), [], [W("r16")])
+    iota(pnum, [[1, 1]], 1)
+    iota(W("rp"), [[1, 64]])
+    iota(W("r16"), [[0, NT], [1, 16]])
     op("v", lambda: g.vector.memset(ap(W("ones")), 1.0), [], [W("ones")])
+    iota(W("r80"), [[64 * NT, 4], [63, NT]])
     op("g", lambda: g.affine_select(ap(W("eb")), ap(W("ones")), [[1, 528]], A.is_equal, 0.0, -3, -4), [W("ones")], [W("eb")])
     for k, m in enumerate((15, 31, 16)):
         ts(col("pj", k), pnum, m, A.bitwise_and)
@@ -233,59 +258,47 @@ def rank_program(g, core, T, topo):
     icol, p32, e16, im1, ip1 = (col("pf", k) for k in range(5))
     ts(col("cl", 0), icol, float(NT), A.mult, float(V), A.add)
     ts(W("nn"), W("rp", 0, 32), 16.0, A.mult, icol, A.add)
-    ts(W("lpi"), W("rp", 0, NT), col("cl", 0), A.add)
     ts(W("lrot", 0, 2), W("rp", 0, 2), 16.0, A.mult, im1, A.add)
-    ts(W("lrot", 2, 4), W("rp", 0, 2), 16.0, A.mult, ip1, A.add)
+    ts(W("lrot", 2, 4), W("rp", 2, 4), 16.0, A.mult, ip1, A.add)
+    ts(W("lpi"), W("rp", 0, NT), col("cl", 0), A.add)
+    ts(W("lrot", 4, 6), W("rp", 0, 2), 16.0, A.mult, im1, A.add)
+    ts(W("lrot", 6, 8), W("rp", 0, 2), 16.0, A.mult, ip1, A.add)
     ts(W("mk"), W("r16"), icol, A.is_equal)
     n4, n24 = W("nn", 0, 4), W("nn", 0, 24)
-    for n in ("ao0", "ap0"):
-        fill(W(n, NT, 32), 0.0)
+    fill(W("sc", 15, SC0, 16), 0.0)
+    fill(W("sc", SC0 + C + 15, SC0 + 512, 16), 0.0)
+    fill(W("bo"), 0.0)
+    ebp = fill(W("bp"), 1.0)
     fill(W("rs"), 0.0)
     fill(W("kp"), 1.0)
-    act(W("k4", 0, 4), n4, AF.Sign, bias=0.5 - V)
-    act(W("k4", 4, 8), n4, AF.Sign, bias=0.5 - V - NT)
-    act(W("k4", 8, 12), W("k4", 0, 4), bias=30.0, scale=-26.0)
-    act(W("k4", 12, 16), W("k4", 4, 8), scale=22.0)
     act(W("nm"), W("mk"), bias=1.0, scale=-1.0)
-    tt(W("k4", 16, 20), W("k4", 8, 12), W("k4", 12, 16), A.add)
-    tt(W("k4", 20, 24), W("k4", 16, 20), n4, A.add)
-    cp(W("lc1"), W("k4", 20, 24))
 
     def list_terms():
-        act(W("k4", 24, 28), n4, bias=-908.0, scale=18.0)
-        act(W("k4", 28, 32), n4, bias=1182.0)
-        act(W("k4", 32, 36), W("k4", 4, 8), scale=-4.0)
-        act(W("k6", 0, 4), n4, AF.Abs, bias=0.5 - NT)
-        act(W("k6", 4, 8), n4, AF.Sign, bias=0.5 - NT)
         act(W("k3", 0, 24), n24, AF.Sign, bias=0.5 - V)
         act(W("k3", 24, 48), n24, AF.Sign, bias=0.5 - V - C)
-        act(W("k6", 8, 12), W("k6", 4, 8), bias=1.5 * NT - 0.5, scale=NT / 2)
-        act(W("k3", 48, 72), W("k3", 0, 24), bias=-16.0 * V, scale=-8.0 * C)
-        act(W("k3", 72, 96), W("k3", 24, 48), scale=-8.0 * C)
         act(W("k3", 96, 120), n24, scale=16.0)
         act(W("k2", 24, 44), W("nn", 0, NT), scale=16.0)
-        fill(W("rs", 0, HK, KW), BIG)
-        fill(W("kp", 0, HK, KW), 0.0)
+        act(W("k3", 48, 72), W("k3", 0, 24), bias=-16.0 * V, scale=-8.0 * C)
+        act(W("k3", 72, 96), W("k3", 24, 48), scale=-8.0 * C)
+        fill(W("rs", 0, QT * KW, KW), BIG)
+        fill(W("kp", 0, HT * KW, KW), 0.0)
 
     def scalar_constants():
-        fill(W("cs", 2 * HK, 1184), 0.0)
-        fill(W("kk"), 1.0)
-        fill(W("ex"), 1.0)
-        act(W("r65"), W("rp"), scale=65.0)
-        act(W("cb"), W("rp", 0, 32), bias=2.0 * V / 64, scale=65.0 / 64)
-        fill(col("kk", NT), 0.0)
-        act(col("cl", 1), icol, bias=64.0 * 401 + 2 * V, scale=64.0 * NT)
-        act(col("cl", 2), icol, bias=64.0 * (400 + C - 2 * NT + 1) + 2 * V, scale=-64.0 * NT)
-        act(col("cl", 3), icol, bias=2.0 * V, scale=float(NT))
+        rt = W("rp", 0, NT)
+        act(W("cb", 0, NT), rt, bias=2.0 * V / 64, scale=65.0 / 64)
+        act(W("cdc"), W("r80"), bias=-130.0 - 2.0 * V / 64, scale=65.0 / 64)
+        act(col("cl", 1), icol, bias=64.0 * C - 2.0 * V / 64, scale=-64.0 * NT)
+        act(col("cl", 2), icol, bias=64.0 - 2.0 * V / 64, scale=64.0 * NT)
+        act(col("cl", 3), icol, scale=float(NT))
         act(col("cl", 4), e16, bias=-8.0, scale=-0.5)
         act(col("cl", 5), e16, bias=0.5, scale=-0.5)
         act(col("cl", 6), e16, bias=-7.5, scale=-1.0)
         act(col("cl", 7), icol, bias=-7.25e6, scale=0.5e6)
         act(col("cl", 8), icol, bias=0.25e6, scale=-0.5e6)
-        act(W("ckb", 0, NT), W("rp", 0, NT), bias=col("cl", 1), scale=64.0)
-        act(W("ckb", NT, 48), W("rp", NT, 48), bias=col("cl", 2), scale=64.0)
-        act(W("cc", 0, NT), W("rp", 0, NT), bias=col("cl", 3))
-        act(W("cc", NT, 48), W("rp", 0, 48 - NT), bias=col("cl", 3))
+        act(W("ckb", 0, NT), rt, bias=col("cl", 1), scale=-64.0 - 65.0 / 64)
+        act(W("ckb", NT, 2 * NT), rt, bias=col("cl", 2), scale=64.0 - 65.0 / 64)
+        act(W("cc", 0, NT), rt, bias=col("cl", 3))
+        act(W("cc", NT, 2 * NT), rt, bias=col("cl", 3))
         act(col("cl", 9), p32, bias=col("cl", 4), scale=-0.5)
         act(col("cl", 10), p32, bias=col("cl", 5), scale=-0.5)
         r32 = W("rp", 0, 32)
@@ -295,41 +308,29 @@ def rank_program(g, core, T, topo):
         act(W("k7", 96, 128), W("k7", 64, 96), AF.Relu, bias=-8.0e6, scale=1.0e6)
         act(W("cz", 0, 32), W("k7", 0, 32), AF.Relu, bias=col("cl", 7), scale=1.0e6)
         act(W("cz", 64, 96), W("k7", 32, 64), AF.Relu, bias=col("cl", 8), scale=1.0e6)
-        act(W("cz", 32, 64), W("k7", 96, 128), bias=64.0 * 400)
-        act(W("cz", 96, 128), W("k7", 96, 128), bias=64.0 * 400)
+        act(W("cz", 32, 64), W("k7", 96, 128), bias=PEN)
+        act(W("cz", 96, 128), W("k7", 96, 128), bias=PEN)
 
     def vector_constants():
-        tt(W("k4", 36, 40), W("k4", 0, 4), W("k4", 4, 8), A.subtract)
-        tt(W("k4", 40, 44), W("k4", 28, 32), W("k4", 32, 36), A.add)
         tt(W("k1", 0, 24), W("k3", 48, 72), W("k3", 72, 96), A.add)
-        tt(W("k4", 44, 48), W("k4", 36, 40), W("k4", 24, 28), A.mult)
-        ts(W("ldup"), W("k6", 0, 4), -1.0, A.mult, NT - 0.5, A.add)
+        ts(W("k5", 48, 52), n4, -2.5, A.add, 1.0 / HT, A.mult)
         tt(W("k2", 0, 24), W("k1", 0, 24), W("k3", 96, 120), A.add)
-        tt(W("k4", 48, 52), W("k4", 44, 48), W("k4", 40, 44), A.add)
-        tt(W("k6", 12, 16), W("k6", 8, 12), W("k6", 0, 4), A.subtract)
+        ts(W("k4", 0, 4), W("k5", 48, 52), 2.0 * NA, A.mult, 2.0, A.add)
         ts(W("k5", 0, 44), W("k2", 0, 44), -8.0 * (NT - 1), A.add, 1.0 / C, A.mult)
-        cp(W("lc2"), W("k4", 48, 52))
-        cp(W("lfin"), W("k6", 12, 16))
+        tt(W("k4", 4, 8), W("k4", 0, 4), n4, A.add)
         ts(W("k1", 0, 44), W("k5", 0, 44), -float(C - 1), A.mult)
+        ts(W("lc"), W("k4", 4, 8), BO - 1.0, A.min)
         tt(W("k9", 0, 44), W("k1", 0, 44), W("k2", 0, 44), A.add)
         cp(W("lnr"), W("k9", 0, 24))
         cp(W("lnf"), W("k9", 24, 44))
-
-    def neighbours(buf, stride, base, t1, t2):
-        return [lambda: tr(W(t1), W(buf, stride - 1, 32 * stride, stride)), lambda: cp(W(t2), W(t1), W("lrot")),
-                lambda: tr(W(buf, base, base + 64), W(t2))]
 
     def weave(chain, fillers):
         for k, f in enumerate(chain):
             f()
             if k < len(fillers):
                 fillers[k]()
-
-    used = topo.mask(core, T.cores[rank ^ STEP[0]])
-
-    def masks(r):
-        full = topo.mask(core, T.cores[rank ^ STEP[r]])
-        return full, full & used
+        for f in fillers[len(chain):]:
+            f()
 
     def scores(r, h):
         a, b = HC * h, HC * h + HC
@@ -338,139 +339,167 @@ def rank_program(g, core, T, topo):
     def mask_scores(h):
         tt(W("sm", HC * h, HC * h + HC), W("pb%d" % h, 0, HC), W("mk", HC * h, HC * h + HC), A.mult)
 
-    def own_scores(a, b):
-        scan(W("sc", a, b), W("nm", a, b), W("sm", a, b), 0.0, A.mult, A.add)
+    def own_scores(h):
+        a, b = HC * h, HC * h + HC
+        scan(W("sc", SC0 + a, SC0 + b), W("nm", a, b), W("sm", a, b), 0.0, A.mult, A.add)
 
-    def send_scores(r, t0, t1, sem):
-        cp(W("ao%d" % r, t0, t1), W("sc", 16 * t0 + 15, 16 * t1, 16))
-        note(None, sem, bin(masks(r)[1]).count("1"), [], [W("ap%d" % r, t0, t1)])
-        remote(T.cores[rank ^ STEP[r]], W("ap%d" % r, t0, t1), W("ao%d" % r, t0, t1), sem, masks(r)[1])
+    def send_scores(r, h):
+        t0, t1 = HT * h, HT * h + HT
+        mine = W("wo", WO * r + 32 + t0, WO * r + 32 + t1)
+        cp(mine, W("sc", SC0 + 16 * t0 + 15, SC0 + 16 * t1, 16))
+        swap(r, ("aw", "ax")[h], W("ap", NT * r + t0, NT * r + t1), mine)
+
+    def ring_q(r, k):
+        a, b = PICK[k]
+        pickq(W("qn%d" % r, 16 * a, 16 * b), W("qp%d" % r), W("lnr", a, b))
+
+    def ring_s(r):
+        for a, b in PICK:
+            picks(W("sn%d" % r, 16 * a, 16 * b), W("sp%d" % r), W("lnr", a, b))
 
     quant(W("qu"), W("su"), W("ut"))
     pickq(W("qur"), W("qu"), W("lu"))
     picks(W("sur"), W("su"), W("lu"))
     list_terms()
     quant(W("qn0", 0, hx), W("sn0", 0, hx), W("x0", 0, 4 * hx))
-    remote(T.cores[rank ^ STEP[0]], W("ls0", 0, hx), W("sn0", 0, hx), "ab0", used)
-    quant(W("qn0", hx, CE), W("sn0", hx, CE), W("x0", 4 * hx, 4 * CE))
+    remote(peer_of(0), W("ls0", 0, hx), W("sn0", 0, hx), "ab0", wide(0))
+    need("g", ebp)
+    quant(W("qn0", hx, CS), W("sn0", hx, CS), W("x0", 4 * hx, 4 * CS))
     for h in range(2):
-        picks(W("sp0", HC * h, HC * h + HC), W("sn0", 0, CE), W("lpi", HT * h, HT * h + HT))
-        pickq(W("qp0", HC * h, HC * h + HC), W("qn0", 0, CE), W("lpi", HT * h, HT * h + HT))
+        picks(W("sp0", HC * h, HC * h + HC), W("sn0", 0, CS), W("lpi", HT * h, HT * h + HT))
+        pickq(W("qp0", HC * h, HC * h + HC), W("qn0", 0, CS), W("lpi", HT * h, HT * h + HT))
         scores(0, h)
     scalar_constants()
     mask_scores(0)
-    own_scores(0, HC)
     mask_scores(1)
-    own_scores(HC, C)
-    send_scores(0, 0, NT, "aw0")
+    own_scores(0)
+    own_scores(1)
+    send_scores(0, 0)
+    send_scores(0, 1)
 
     for r in range(R):
-        peer = T.cores[rank ^ STEP[r]]
-        full = masks(r)[0]
-        qp, sp, qn, sn = "qp%d" % r, "sp%d" % r, "qn%d" % r, "sn%d" % r
-        wo, wp, lq, ls, ao, pa = "wo%d" % r, "wp%d" % r, "lq%d" % r, "ls%d" % r, "ao%d" % r, "ap%d" % r
-        note(None, "ab%d" % r, (2 if r else 3) * bin(full).count("1"), [], [W(lq), W(ls)])
-        chain = neighbours(ao, 1, 32, "t1", "t2") + [lambda: cp(W(wo), W(ao), W("lc1"))]
+        peer = peer_of(r)
+        qp, sp, qn, sn, lq, ls = ("%s%d" % (n, r) for n in ("qp", "sp", "qn", "sn", "lq", "ls"))
+        wo, bo, bp = WO * r, BO * r, BP * r
+        note(None, "ab%d" % r, (2 if r else 3) * bin(wide(r)).count("1"), [], [W(lq), W(ls)])
+
+        def turn_scores():
+            tr(W("t1", 0, 32), W("sc", 15, 512, 16))
+            tr(W("t1", 32, 64), W("sc", SC0 + 15, SC0 + 512, 16))
+
+        def turn_back():
+            tr(W("wo", wo, wo + 32), W("t2", 0, 32))
+            tr(W("wo", wo + 32 + NT, wo + 64 + NT), W("t2", 32, 64))
+
+        chain = [turn_scores, lambda: cp(W("t2"), W("t1"), W("lrot", 0, 4)), turn_back]
         if r > 0:
-            for a, b in PICK:
-                picks(W(sn, 16 * a, 16 * b), W(sp), W("lnr", a, b))
-            weave(chain, [lambda a=a, b=b: pickq(W(qn, 16 * a, 16 * b), W(qp), W("lnr", a, b)) for a, b in PICK])
+            weave(chain, [lambda: None, lambda: ring_q(r, 1), lambda: ring_q(r, 2)])
         else:
             weave(chain, [lambda b=b: quant(blk("qe", b), blk("se", b), W("eb", 3 - b, 515 - b)) for b in range(4)])
-        remote(peer, W(lq), W(qn, 0, CE), "ab%d" % r, full, True)
+        remote(peer, W(lq), W(qn, 0, CS), "ab%d" % r, wide(r), True)
         s0 = 0 if r else hx
-        remote(peer, W(ls, s0, CE), W(sn, s0, CE), "ab%d" % r, full)
+        remote(peer, W(ls, s0, CS), W(sn, s0, CS), "ab%d" % r, wide(r))
         if r == 0:
             vector_constants()
         for b in range(4):
             mx(W("pb%d" % (4 + b), 0, C), blk("qe", b), blk("se", b), W(qp), W(sp))
         for b in range(4):
-            mx(W("pb%d" % b, 0, CE), blk("qe", b), blk("se", b), W(lq), W(ls))
+            mx(W("pb%d" % b, 0, CS), blk("qe", b), blk("se", b), W(lq), W(ls))
 
-        def seg(name, s):
-            return W(name, KW * s, KW * s + KW)
+        def seg(name, t0, t1=None):
+            return W(name, KW * t0, KW * (t0 + 1 if t1 is None else t1))
 
-        def half(name, k):
-            return W(name, HK * k, HK * k + HK)
+        def ends(name, t0, t1):
+            return W(name, KW * t0 + KW - 1, KW * t1, KW)
 
-        def least(k, t0=0, t1=HT):
-            a, b = HK * k + KW * t0, HK * k + KW * t1
-            scan(W("mm", a, b), W("rs", 0, b - a), W("dd", a, b), 0.0, A.max, A.min)
+        def least(k):
+            scan(seg("mm", QT * k, QT * k + QT), W("rs"), seg("dd", QT * k, QT * k + QT), 0.0, A.max, A.min)
 
-        def above(t):
-            ts(seg("fl", t), seg("mm", t), col("mm", KW * t + KW - 1), A.is_gt)
+        def above(t0, t1):
+            for t in range(t0, t1):
+                ts(seg("fl", t), seg("mm", t), col("mm", KW * t + KW - 1), A.is_gt)
 
-        def tally(k):
-            scan(half("cs", k), W("kp"), half("fl", k), 0.0, A.mult, A.add)
+        def tally(t0, t1):
+            scan(seg("cs", t0, t1), seg("kp", 0, t1 - t0), seg("fl", t0, t1), 0.0, A.mult, A.add)
 
-        def signs(k):
-            for t in range(HT * k, HT * k + HT):
-                s = seg("mm", NT + t)
-                act(seg("jk", t), s, AF.Sign, bias=col("mm", s[2] - 1), scale=-1.0, acc=col("nd", t))
+        b0 = bo + 32 + 2 * NA
+        nv = NT - NS
+
+        def bcol(base, t):
+            return base + t + (2 * NA if t >= HT else 0)
 
         for t in range(NT):
-            act(seg("dd", t), W(wo, t, t + KW), AF.Abs, bias=col(pa, t), scale=-1.0)
-        chain = neighbours(pa, 1, 32, "t1", "t2") + [lambda: cp(W(wp), W(pa), W("lc1"))]
-        if r > 0:
-            least(0, 0, 5)
-            least(0, 5, HT)
-            weave(chain, [lambda t=t: above(t) for t in range(3)])
-        else:
-            weave(chain, [])
-        for t in range(NT):
-            act(seg("dd", NT + t), W(wp, t, t + KW), AF.Abs, bias=col(ao, t), scale=-1.0)
-        if r == 0:
-            least(0)
-        for t in range(3 if r else 0, HT):
-            above(t)
+            act(seg("dd", t), W("wo", wo + 32 - V + t, wo + 32 + V + 1 + t), AF.Abs, bias=col("ap", NT * r + t), scale=-1.0)
+        least(0)
+        above(0, 2)
         least(1)
-        if r > 0:
-            tally(0)
+        above(2, QT)
         least(2)
-        signs(0)
-        if r == 0:
-            tally(0)
-        for t in range(HT, NT):
-            above(t)
-        least(3, 0, 5)
-        tally(1)
-        least(3, 5, HT)
-        signs(1)
-        weave(neighbours("cs", KW, 1184, "t1b", "t2b") + [lambda: tt(W("cd"), W("cs"), W("r65"), A.add, W("lc2"))],
-              [lambda: tt(W("bi", 0, HT), W("nd", 0, HT), W("cb", 0, HT), A.subtract),
-               lambda: ts(W("ex", 0, HT), W("nd", 0, HT), 2.0, A.mult, 2.0 * V, A.add)])
-        nka = NT - NKD
+        above(QT, 8)
+        least(3)
+        above(8, HT)
+        tally(0, HT)
+        for t in range(nv, NT):
+            act(seg("jk", t), seg("mm", t), AF.Sign, bias=col("mm", KW * t + KW - 1), scale=-1.0, acc=col("nd", t))
+        tt(W("bo", b0, b0 + HT), ends("cs", 0, HT), W("cb", 0, HT), A.add)
+        ts(W("bo", b0 + HT, b0 + HT + NA), ends("cs", 0, NA), 2.0, A.mult, -2.0 * V, A.add)
+        swap(r, "ay", W("bp", bp, bp + HT + NA), W("bo", b0, b0 + HT + NA))
+        if nv > HT:
+            above(HT, nv)
+            tally(HT, nv)
+            tt(W("bo", bcol(b0, HT), bcol(b0, nv)), ends("cs", HT, nv), W("cb", HT, nv), A.add)
+        act(W("bo", b0 + HT + NA, b0 + HT + 2 * NA), W("nd", NT - NA, NT), bias=-2.0 * V, scale=-2.0)
+        tt(W("bo", bcol(b0, nv), bcol(b0, NT)), W("cb", nv, NT), W("nd", nv, NT), A.subtract)
+        swap(r, "az", W("bp", bp + BP - HT - NA, bp + BP), W("bo", b0 + HT + NA, b0 + 32))
+        tr(W("t3"), W("bo", b0, b0 + 32))
+        cp(W("t4"), W("t3"), W("lrot", 4, 8))
+        tr(W("bo", bo, bo + 32), W("t4", 0, 32))
+        tr(W("bo", bo + BO - 32, bo + BO), W("t4", 32, 64))
+        tt(W("cd"), W("bo", bo, bo + BO), W("cdc", 2, 66), A.add, W("lc"))
 
-        def back(t):
-            act(seg("jk", t), W("cd", t, t + KW), AF.Sign, bias=col("bi", t), scale=1.0 / 64, acc=col("ks", KW * t + KW - 1))
+        def mine(t):
+            return bp + t + (NT if t >= HT else 0)
 
-        for t in range(HT):
-            back(t)
-        tt(W("bi", HT, NT), W("nd", HT, NT), W("cb", HT, NT), A.subtract)
-        for t in range(HT, nka):
-            back(t)
-        tt(W("kb"), W("nd", 0, NT), W("ckb"), A.add, W("ldup", 0, 3))
-        for t in range(nka, NT):
-            ts(seg("f2", t - nka), W("cd", t, t + KW), -1.0 / 64, A.mult, col("bi", t), A.is_equal)
-        ts(W("ex", HT, nka), W("nd", HT, nka), 2.0, A.mult, 2.0 * V, A.add)
-        scan(W("ks", KW * nka, 2 * HK), W("kp", 0, KW * NKD), W("f2", 0, KW * NKD), 0.0, A.mult, A.add)
+        def back(t0, t1):
+            for t in range(t0, t1):
+                act(seg("jk", t), W("cd", t, t + KW), AF.Sign, bias=col("bp", mine(t)), scale=-1.0 / 64, acc=col("ks", KW * t + KW - 1))
+
+        def hits(t0, t1):
+            for t in range(t0, t1):
+                ts(seg("f2", t), W("cd", t, t + KW), 1.0 / 64, A.mult, col("bp", mine(t)), A.is_equal)
+
+        def keys(t0, t1):
+            for k in range(2):
+                tt(W("kb", NT * k + t0, NT * k + t1), W("bp", mine(t0), mine(t0) + t1 - t0), W("ckb", NT * k + t0, NT * k + t1), A.add)
+
+        def sums(t0, t1):
+            scan(seg("ks", t0, t1), seg("kp", 0, t1 - t0), seg("f2", t0, t1), 0.0, A.mult, A.add)
+
+        back(0, NA)
+        hits(NA, HT)
+        keys(0, HT)
+        sums(NA, HT)
+        back(NT - NA, NT)
+        hits(HT, NT - NA)
+        keys(HT, NT)
+        sums(HT, NT - NA)
         for b in range(4):
-            act(W("psb", PW * b, PW * b + CE), W("pb%d" % b, 0, CE), scale=0.5)
-        tt(W("ok", 0, NT), W("ks", KW - 1, 2 * HK, KW), W("ex", 0, NT), A.is_equal)
-        tt(W("ky"), W("ok", 0, NT), W("kb"), A.mult, W("ldup", 0, 3))
-        scan(W("lo"), W("kk"), W("ky"), 0.0, A.mult, A.max)
-        ts(W("zz", 0, 32), W("cz", 0, 32), -1.0, A.mult, col("lo", NT - 1), A.add)
-        ts(W("zz", 32, 96), W("cz", 32, 96), -1.0, A.mult, col("lo", 2 * NT - 1), A.add)
-        ts(W("zz", 96, 128), W("cz", 96, 128), -1.0, A.mult, col("lo", NT - 1), A.add)
+            act(W("psb", PW * b, PW * b + CS), W("pb%d" % b, 0, CS), scale=0.5)
+            act(W("psb", PW * b + CS, PW * b + CE), W("pb%d" % b, V, 2 * V), scale=0.5)
+        tt(W("no", 0, NT), ends("ks", 0, NT), W("bp", bp + HT, bp + HT + NT), A.not_equal)
+        scan(W("lo", 0, NT), W("no", 0, NT), W("kb", 0, NT), NONE, A.mult, A.max)
+        scan(back_to_front(W("lo", NT, 2 * NT)), back_to_front(W("no", 0, NT)), back_to_front(W("kb", NT, 2 * NT)), NONE, A.mult, A.max)
+        ts(W("zz", 0, 32), W("cz", 0, 32), col("lo", NT - 1), A.add, DEF, A.min)
+        ts(W("zz", 96, 128), W("cz", 96, 128), col("lo", NT - 1), A.add, DEF, A.min)
+        ts(W("zz", 32, 96), W("cz", 32, 96), col("lo", NT), A.add, DEF, A.min)
         tr(W("zt"), W("zz"))
-        red(col("cl", 12), W("zt", 0, 64))
         red(col("cl", 13), W("zt", 64, 128))
-        ts(W("fi", 0, NT), W("lo", 0, NT), col("cl", 12), A.max, float(V), A.max)
-        ts(W("fi", NT, 2 * NT), W("lo", NT, 2 * NT), col("cl", 13), A.max, float(V), A.max)
+        red(col("cl", 12), W("zt", 0, 64))
+        ts(W("fi", NT, 2 * NT), W("lo", NT, 2 * NT), col("cl", 13), A.min)
+        ts(W("fi", 0, NT), W("lo", 0, NT), col("cl", 12), A.min)
         ts(W("lw", 0, 2 * NT), W("fi", 0, 2 * NT), 63, A.bitwise_and)
-        tt(W("na"), W("lw", 0, 2 * NT), W("cc", 0, 48), A.subtract, W("lfin", 0, 3))
-        ts(W("off", NT, 2 * NT), W("na", NT, 2 * NT), -1.0, A.mult)
-        ts(W("off", 0, NT), W("na", 0, NT), -1.0, A.mult)
+        tt(W("na", 0, 2 * NT), W("lw", 0, 2 * NT), W("cc", 0, 2 * NT), A.add)
+        cp(W("off", 0, 2 * NT), W("na", 0, 2 * NT))
         nq, ns = "qp%d" % (r + 1), "sp%d" % (r + 1)
 
         def plane(b):
@@ -490,8 +519,8 @@ def rank_program(g, core, T, topo):
                 mx(W("pb%d" % b, 0, HC), blk("qw", b), blk("sw", b), W("qy", a, a + HC), W("sy", a, a + HC))
                 act(part("rl", b, h), W("pb%d" % b, 0, HC), AF.Relu, scale=0.03125)
 
-        def state(h, b0, b1):
-            for b in range(b0, b1):
+        def state(h, b0_, b1_):
+            for b in range(b0_, b1_):
                 tt(W("xt", 4 * HC * h + b, 4 * HC * (h + 1), 4), part("rl", b, h), W("pb%d" % (4 + b), HC * h, HC * h + HC), A.add)
 
         def pack(h):
@@ -505,9 +534,7 @@ def rank_program(g, core, T, topo):
                 else:
                     act(part("hb", b, h), plane(b), AF.Copy, ind=hoff)
         if r == R - 1:
-            tt(W("odt"), W("cc", 48, 96), W("na"), A.subtract)
-            dma("s", T.od[:, 0:C], T.odt[:, 0:NT], [W("odt")], [])
-            dma("s", T.od[:, C:2 * C], T.odt[:, NT:2 * NT], [W("odt")], [])
+            act(W("odt", 0, 2 * NT), W("na", 0, 2 * NT), bias=-float(V))
         for b in (1, 0, 2, 3):
             fetch(0, b)
         fetch(1, 0)
@@ -516,28 +543,29 @@ def rank_program(g, core, T, topo):
             fetch(1, b)
         state(0, 0, 1)
         layer(1)
-        if r == 0:
-            for k in range(1, R):
-                fill(W("ao%d" % k, NT, 32), 0.0)
-                fill(W("ap%d" % k, NT, 32), 0.0)
-            act(W("cc", 48, 96), W("cc", 0, 48), bias=float(V), scale=-1.0)
         state(0, 1, 4)
         if r == 0:
             quant(W("qv"), W("sv"), W("vt"))
+        if r == R - 1:
+            tt(W("odt", 0, 2 * NT), W("odt", 0, 2 * NT), W("cc", 0, 2 * NT), A.subtract)
+            dma("s", T.od[:, 0:C], T.odt[:, 0:NT], [W("odt")], [])
+            dma("s", T.od[:, C:2 * C], T.odt[:, NT:2 * NT], [W("odt")], [])
         pack(0)
         if r < R - 1:
             scores(r + 1, 0)
             state(1, 0, 2)
             mask_scores(0)
             state(1, 2, 3)
-            own_scores(0, HC)
+            own_scores(0)
             state(1, 3, 4)
-            send_scores(r + 1, 0, HT, "aw%d" % (r + 1))
+            send_scores(r + 1, 0)
             pack(1)
             scores(r + 1, 1)
+            ring_s(r + 1)
+            ring_q(r + 1, 0)
             mask_scores(1)
-            own_scores(HC, C)
-            send_scores(r + 1, HT, NT, "ax%d" % (r + 1))
+            own_scores(1)
+            send_scores(r + 1, 1)
         else:
             state(1, 0, 4)
             pack(1)

from concourse.mybir import dt, AluOpType, AxisListType, ActivationFunctionType

C, V, R = 320, 18, 3
STEP = [1, 2, 1]
NT = C // 16
KW = 2 * V + 1
HT = NT // 2
QT = NT // 4
HC = C // 2
CS = C + V
CE = C + 2 * V
PW = 368
QW = 352
NS = 10
NA = 6
PICK = [(0, 8), (8, 14), (14, 22)]
SC0 = 16 * (32 - NT)
WO, BO, BP = 96, 120, 40
BIG = 1.0e29
NONE, PEN, DEF = 64.0 * 1000, 64.0 * 400, 64.0 * 800 + V
F32, BF, I32, U16, Q4, U8 = "float32", "bfloat16", "int32", "uint16", "float8_e4m3fn_x4", "uint8"

_SB = {
    "x0": (4 * CS, BF), "ut": (512, BF), "vt": (512, BF), "ones": (528, BF), "eb": (528, BF),
    "qu": (128, Q4), "su": (128, U8), "qur": (128, Q4), "sur": (128, U8), "qv": (128, Q4), "sv": (128, U8),
    "qw": (512, Q4), "sw": (512, U8), "qe": (512, Q4), "se": (512, U8), "qy": (C, Q4), "sy": (C, U8),
    "xt": (4 * C, BF), "yt": (4 * C, BF), "hb": (4 * C, BF), "rl": (4 * C, F32), "psb": (4 * PW, BF),
    "pj": (8, I32), "pf": (8, F32), "cl": (16, F32), "rp": (64, F32), "r16": (C, F32), "r80": (80, F32),
    "mk": (C, F32), "nm": (C, F32), "sm": (C, F32), "sc": (SC0 + 512, F32), "t1": (64, F32), "t2": (64, F32),
    "t3": (32, F32), "t4": (64, F32),
    "dd": (NT * KW, F32), "mm": (NT * KW, F32), "rs": (QT * KW, F32), "kp": (HT * KW, BF), "fl": (NT * KW, BF),
    "f2": (NT * KW, BF), "cs": (NT * KW, BF), "cd": (64, F32), "cdc": (80, F32),
    "nd": (32, F32), "cb": (32, F32), "ks": (NT * KW, F32), "jk": (NT * KW, BF),
    "no": (32, F32), "kb": (48, F32), "ckb": (48, F32), "lo": (48, F32),
    "zz": (128, F32), "cz": (128, F32), "zt": (128, F32), "fi": (48, I32), "lw": (48, I32),
    "cc": (48, F32), "na": (48, F32), "off": (48, U16), "odt": (48, F32), "yo": (C, F32),
    "lpi": (20, U16), "lu": (8, U16), "lrot": (8, U16), "lc": (4, U16), "lnr": (24, U16), "lnf": (20, U16),
    "k1": (64, F32), "k2": (64, F32), "k3": (128, F32), "k4": (64, F32), "k5": (64, I32),
    "k7": (128, F32), "k9": (64, F32), "nn": (32, F32),
    "wo": (R * WO, F32), "ap": (R * NT, F32), "bo": (R * BO, F32), "bp": (R * BP, F32),
}
for _r in range(R + 1):
    _SB["qn%d" % _r] = (QW, Q4)
    _SB["sn%d" % _r] = (QW, U8)
    _SB["qp%d" % _r] = (C, Q4)
    _SB["sp%d" % _r] = (C, U8)
for _r in range(R):
    _SB["lq%d" % _r] = (CS, Q4)
    _SB["ls%d" % _r] = (CS, U8)
SCRATCH = {k: ("sbuf", [128, n], d) for k, (n, d) in _SB.items()}
for _b in range(8):
    SCRATCH["pb%d" % _b] = ("psum", [128, 512], F32)
NDMA = 20
SEMAPHORES = (["cv", "ca", "ct", "cg", "sent"] + ["dm%d" % k for k in range(NDMA)]
              + ["%s%d" % (n, k) for k in range(R) for n in ("aw", "ax", "ay", "az", "ab")])

A = AluOpType
AF = ActivationFunctionType


def rank_program(g, core, T, topo):
    rank = T.rank_of(core)
    if rank is None:
        return
    eng = {"v": g.vector, "a": g.scalar, "t": g.tensor, "g": g, "s": g.sync}
    csem = {"v": "cv", "a": "ca", "t": "ct", "g": "cg"}
    count = {}
    known = {q: {} for q in eng}
    events = []
    lastw = {}
    reads = {}
    bank = {}
    ndma = [0]

    def cols(v):
        return range(v[1], v[2], v[3])

    def W(name, a=0, b=None, s=1):
        return (name, a, SCRATCH[name][1][1] if b is None else b, s)

    def back_to_front(v):
        return (v[0], v[2] - 1, v[1] - 1, -1)

    def ap(v):
        if v[3] == 1:
            return T[v[0]][:, v[1]:v[2]]
        return T[v[0]][:, v[1]:(v[2] if v[2] >= 0 else None):v[3]]

    def need(q, e):
        sem, val_, clk = events[e][0], events[e][1], events[e][2]
        if known[q].get(sem, 0) >= val_:
            return
        eng[q].wait_ge(T.sem[sem], val_)
        for s, n in clk.items():
            if known[q].get(s, 0) < n:
                known[q][s] = n
        known[q][sem] = val_

    def order(q, rd, wr):
        deps = set()
        for v in rd:
            lw_ = lastw.setdefault(v[0], {})
            deps.update(lw_[c] for c in cols(v) if c in lw_)
        for v in wr:
            lw_ = lastw.setdefault(v[0], {})
            rr = reads.setdefault(v[0], {})
            for c in cols(v):
                if c in lw_:
                    deps.add(lw_[c])
                deps.update(rr.get(c, ()))
        for v in rd + wr:
            if SCRATCH[v[0]][0] == "psum":
                deps.update(e for e in bank.get(v[0], []) if events[e][3] != q)
        for e in sorted(deps, reverse=True):
            need(q, e)

    def note(q, sem, n, rd, wr):
        count[sem] = count.get(sem, 0) + n
        e = len(events)
        events.append((sem, count[sem], dict(known[q]) if q else {}, q))
        for v in rd:
            rr = reads.setdefault(v[0], {})
            for c in cols(v):
                rr.setdefault(c, []).append(e)
        for v in wr:
            lw_ = lastw.setdefault(v[0], {})
            rr = reads.setdefault(v[0], {})
            for c in cols(v):
                lw_[c] = e
                rr.pop(c, None)
        for v in rd + wr:
            if SCRATCH[v[0]][0] == "psum":
                bank[v[0]] = [x for x in bank.get(v[0], []) if events[x][3] == q] + [e]
        return e

    def op(q, fn, rd, wr):
        order(q, rd, wr)
        fn().then_inc(T.sem[csem[q]], 1)
        return note(q, csem[q], 1, rd, wr)

    def dma(q, out, in_, rd, wr):
        order(q, rd, wr)
        sem = "dm%d" % ndma[0]
        ndma[0] += 1
        eng[q].dma_start(out, in_).then_inc(T.sem[sem], 16)
        return note(q, sem, 16, rd, wr)

    def views(*xs):
        return [x for x in xs if isinstance(x, tuple)]

    def val(x):
        return ap(x) if isinstance(x, tuple) else x

    def src(v, ind):
        return ap(v) if ind is None else ap(v).indirect(ap(ind))

    def cp(o, i, ind=None):
        return op("v", lambda: g.vector.tensor_copy(ap(o), src(i, ind)), views(i, ind), [o])

    def tt(o, a, b, f, ind=None):
        return op("v", lambda: g.vector.tensor_tensor(ap(o), src(a, ind), ap(b), f), views(a, b, ind), [o])

    def ts(o, a, s1, f1, s2=None, f2=None):
        if f2 is None:
            return op("v", lambda: g.vector.tensor_scalar(ap(o), ap(a), val(s1), None, f1), views(a, s1), [o])
        return op("v", lambda: g.vector.tensor_scalar(ap(o), ap(a), val(s1), val(s2), f1, f2), views(a, s1, s2), [o])

    def scan(o, a, b, init, f0, f1):
        return op("v", lambda: g.vector.tensor_tensor_scan(ap(o), ap(a), ap(b), init, f0, f1), [a, b], [o])

    def tr(o, i):
        return op("v", lambda: g.vector.transpose(ap(o), ap(i)), [i], [o])

    def red(o, i):
        return op("v", lambda: g.vector.tensor_reduce(ap(o), ap(i), AxisListType.X, A.min), [i], [o])

    def act(o, i, f=AF.Identity, bias=None, scale=None, acc=None, ind=None):
        kw = {}
        if bias is not None:
            kw["bias"] = val(bias)
        if scale is not None:
            kw["scale"] = scale
        if acc is not None:
            kw["accum_out"] = ap(acc)
        return op("a", lambda: g.scalar.activation(ap(o), src(i, ind), f, **kw), views(i, bias, ind), views(o, acc))

    def fill(o, c):
        return act(o, W("ones", 0, len(cols(o))), scale=float(c))

    def quant(q, s, i):
        return op("v", lambda: g.vector.quantize_mx(ap(q), ap(s), ap(i)), [i], [q, s])

    def mx(o, lq_, ls_, rq, rs_):
        return op("t", lambda: g.tensor.matmul_mx(ap(o), ap(lq_), ap(ls_), ap(rq), ap(rs_), True, True), [lq_, ls_, rq, rs_], [o])

    def pickq(o, i, ind):
        return op("v", lambda: g.vector.tensor_copy(ap(o).bitcast(dt.uint32), ap(i).bitcast(dt.uint32).indirect(ap(ind))), [i, ind], [o])

    def picks(o, i, ind):
        return act(o, i, AF.Copy, ind=ind)

    def iota(o, pattern, mult=0):
        if SCRATCH[o[0]][2] == I32:
            return op("g", lambda: g.iota(ap(o), pattern, 0, mult), [], [o])
        return op("g", lambda: g.iota(ap(o), pattern, 0, mult, allow_small_or_imprecise_dtypes=True), [], [o])

    def remote(peer, o, i, sem, mask, codes=False):
        order("g", [i], [])
        rid, pid = topo.addr(peer)[0], topo.addr(peer)[1]
        oa, ia = ap(o), ap(i)
        if codes:
            oa, ia = oa.bitcast(dt.uint8), ia.bitcast(dt.uint8)
        g.remote_dma(oa, ia, T.sem[sem], T.sem["sent"], pid, rid, mask)
        count["sent"] = count.get("sent", 0) + bin(mask).count("1")

    def col(name, c):
        return W(name, c, c + 1)

    def blk(name, b):
        return W(name, 128 * b, 128 * b + 128)

    def peer_of(r):
        return T.cores[rank ^ STEP[r]]

    short = topo.mask(core, peer_of(0))

    def wide(r):
        return (topo.mask(core, peer_of(r)) & ~short) or short

    def swap(r, sem, land, out):
        note(None, "%s%d" % (sem, r), bin(short).count("1"), [], [land])
        remote(peer_of(r), land, out, "%s%d" % (sem, r), short)

    hx = V + HC
    dma("a", T.ut[:], T.u[:], [], [W("ut")])
    dma("s", T.x0[:, 4 * V:4 * hx], T.x[:, 0:4 * HC], [], [W("x0", 4 * V, 4 * hx)])
    dma("a", T.x0[:, 0:4 * V], T.x[:, 4 * (C - V):4 * C], [], [W("x0", 0, 4 * V)])
    ex0 = dma("s", T.x0[:, 4 * hx:4 * CS], T.x[:, 4 * HC:4 * C], [], [W("x0", 4 * hx, 4 * CS)])
    need("s", ex0)
    dma("s", T.qw[:].bitcast(dt.uint8), T.wc[:], [], [W("qw")])
    dma("s", T.sw[:], T.ws[:], [], [W("sw")])
    dma("s", T.vt[:], T.v[:], [], [W("vt")])

    pnum = col("pj", 7)
    iota(pnum, [[1, 1]], 1)
    iota(W("rp"), [[1, 64]])
    iota(W("r16"), [[0, NT], [1, 16]])
    op("v", lambda: g.vector.memset(ap(W("ones")), 1.0), [], [W("ones")])
    iota(W("r80"), [[64 * NT, 4], [63, NT]])
    op("g", lambda: g.affine_select(ap(W("eb")), ap(W("ones")), [[1, 528]], A.is_equal, 0.0, -3, -4), [W("ones")], [W("eb")])
    for k, m in enumerate((15, 31, 16)):
        ts(col("pj", k), pnum, m, A.bitwise_and)
    ts(col("pj", 5), pnum, 15, A.add)
    ts(col("pj", 6), pnum, 1, A.add)
    ts(W("lu"), W("rp", 0, 8), 16.0, A.mult)
    ts(W("pj", 3, 5), W("pj", 5, 7), 15, A.bitwise_and)
    cp(W("pf", 0, 5), W("pj", 0, 5))
    icol, p32, e16, im1, ip1 = (col("pf", k) for k in range(5))
    ts(col("cl", 0), icol, float(NT), A.mult, float(V), A.add)
    ts(W("nn"), W("rp", 0, 32), 16.0, A.mult, icol, A.add)
    ts(W("lrot", 0, 2), W("rp", 0, 2), 16.0, A.mult, im1, A.add)
    ts(W("lrot", 2, 4), W("rp", 2, 4), 16.0, A.mult, ip1, A.add)
    ts(W("lpi"), W("rp", 0, NT), col("cl", 0), A.add)
    ts(W("lrot", 4, 6), W("rp", 0, 2), 16.0, A.mult, im1, A.add)
    ts(W("lrot", 6, 8), W("rp", 0, 2), 16.0, A.mult, ip1, A.add)
    ts(W("mk"), W("r16"), icol, A.is_equal)
    n4, n24 = W("nn", 0, 4), W("nn", 0, 24)
    fill(W("sc", 15, SC0, 16), 0.0)
    fill(W("sc", SC0 + C + 15, SC0 + 512, 16), 0.0)
    fill(W("bo"), 0.0)
    ebp = fill(W("bp"), 1.0)
    fill(W("rs"), 0.0)
    fill(W("kp"), 1.0)
    act(W("nm"), W("mk"), bias=1.0, scale=-1.0)

    def list_terms():
        act(W("k3", 0, 24), n24, AF.Sign, bias=0.5 - V)
        act(W("k3", 24, 48), n24, AF.Sign, bias=0.5 - V - C)
        act(W("k3", 96, 120), n24, scale=16.0)
        act(W("k2", 24, 44), W("nn", 0, NT), scale=16.0)
        act(W("k3", 48, 72), W("k3", 0, 24), bias=-16.0 * V, scale=-8.0 * C)
        act(W("k3", 72, 96), W("k3", 24, 48), scale=-8.0 * C)
        fill(W("rs", 0, QT * KW, KW), BIG)
        fill(W("kp", 0, HT * KW, KW), 0.0)

    def scalar_constants():
        rt = W("rp", 0, NT)
        act(W("cb", 0, NT), rt, bias=2.0 * V / 64, scale=65.0 / 64)
        act(W("cdc"), W("r80"), bias=-130.0 - 2.0 * V / 64, scale=65.0 / 64)
        act(col("cl", 1), icol, bias=64.0 * C - 2.0 * V / 64, scale=-64.0 * NT)
        act(col("cl", 2), icol, bias=64.0 - 2.0 * V / 64, scale=64.0 * NT)
        act(col("cl", 3), icol, scale=float(NT))
        act(col("cl", 4), e16, bias=-8.0, scale=-0.5)
        act(col("cl", 5), e16, bias=0.5, scale=-0.5)
        act(col("cl", 6), e16, bias=-7.5, scale=-1.0)
        act(col("cl", 7), icol, bias=-7.25e6, scale=0.5e6)
        act(col("cl", 8), icol, bias=0.25e6, scale=-0.5e6)
        act(W("ckb", 0, NT), rt, bias=col("cl", 1), scale=-64.0 - 65.0 / 64)
        act(W("ckb", NT, 2 * NT), rt, bias=col("cl", 2), scale=64.0 - 65.0 / 64)
        act(W("cc", 0, NT), rt, bias=col("cl", 3))
        act(W("cc", NT, 2 * NT), rt, bias=col("cl", 3))
        act(col("cl", 9), p32, bias=col("cl", 4), scale=-0.5)
        act(col("cl", 10), p32, bias=col("cl", 5), scale=-0.5)
        r32 = W("rp", 0, 32)
        act(W("k7", 64, 96), r32, AF.Abs, bias=col("cl", 6))
        act(W("k7", 0, 32), r32, AF.Abs, bias=col("cl", 9))
        act(W("k7", 32, 64), r32, AF.Abs, bias=col("cl", 10))
        act(W("k7", 96, 128), W("k7", 64, 96), AF.Relu, bias=-8.0e6, scale=1.0e6)
        act(W("cz", 0, 32), W("k7", 0, 32), AF.Relu, bias=col("cl", 7), scale=1.0e6)
        act(W("cz", 64, 96), W("k7", 32, 64), AF.Relu, bias=col("cl", 8), scale=1.0e6)
        act(W("cz", 32, 64), W("k7", 96, 128), bias=PEN)
        act(W("cz", 96, 128), W("k7", 96, 128), bias=PEN)

    def vector_constants():
        tt(W("k1", 0, 24), W("k3", 48, 72), W("k3", 72, 96), A.add)
        ts(W("k5", 48, 52), n4, -2.5, A.add, 1.0 / HT, A.mult)
        tt(W("k2", 0, 24), W("k1", 0, 24), W("k3", 96, 120), A.add)
        ts(W("k4", 0, 4), W("k5", 48, 52), 2.0 * NA, A.mult, 2.0, A.add)
        ts(W("k5", 0, 44), W("k2", 0, 44), -8.0 * (NT - 1), A.add, 1.0 / C, A.mult)
        tt(W("k4", 4, 8), W("k4", 0, 4), n4, A.add)
        ts(W("k1", 0, 44), W("k5", 0, 44), -float(C - 1), A.mult)
        ts(W("lc"), W("k4", 4, 8), BO - 1.0, A.min)
        tt(W("k9", 0, 44), W("k1", 0, 44), W("k2", 0, 44), A.add)
        cp(W("lnr"), W("k9", 0, 24))
        cp(W("lnf"), W("k9", 24, 44))

    def weave(chain, fillers):
        for k, f in enumerate(chain):
            f()
            if k < len(fillers):
                fillers[k]()
        for f in fillers[len(chain):]:
            f()

    def scores(r, h):
        a, b = HC * h, HC * h + HC
        mx(W("pb%d" % h, 0, HC), W("qur"), W("sur"), W("qp%d" % r, a, b), W("sp%d" % r, a, b))

    def mask_scores(h):
        tt(W("sm", HC * h, HC * h + HC), W("pb%d" % h, 0, HC), W("mk", HC * h, HC * h + HC), A.mult)

    def own_scores(h):
        a, b = HC * h, HC * h + HC
        scan(W("sc", SC0 + a, SC0 + b), W("nm", a, b), W("sm", a, b), 0.0, A.mult, A.add)

    def send_scores(r, h):
        t0, t1 = HT * h, HT * h + HT
        mine = W("wo", WO * r + 32 + t0, WO * r + 32 + t1)
        cp(mine, W("sc", SC0 + 16 * t0 + 15, SC0 + 16 * t1, 16))
        swap(r, ("aw", "ax")[h], W("ap", NT * r + t0, NT * r + t1), mine)

    def ring_q(r, k):
        a, b = PICK[k]
        pickq(W("qn%d" % r, 16 * a, 16 * b), W("qp%d" % r), W("lnr", a, b))

    def ring_s(r):
        for a, b in PICK:
            picks(W("sn%d" % r, 16 * a, 16 * b), W("sp%d" % r), W("lnr", a, b))

    quant(W("qu"), W("su"), W("ut"))
    pickq(W("qur"), W("qu"), W("lu"))
    picks(W("sur"), W("su"), W("lu"))
    list_terms()
    quant(W("qn0", 0, hx), W("sn0", 0, hx), W("x0", 0, 4 * hx))
    remote(peer_of(0), W("ls0", 0, hx), W("sn0", 0, hx), "ab0", wide(0))
    need("g", ebp)
    quant(W("qn0", hx, CS), W("sn0", hx, CS), W("x0", 4 * hx, 4 * CS))
    for h in range(2):
        picks(W("sp0", HC * h, HC * h + HC), W("sn0", 0, CS), W("lpi", HT * h, HT * h + HT))
        pickq(W("qp0", HC * h, HC * h + HC), W("qn0", 0, CS), W("lpi", HT * h, HT * h + HT))
        scores(0, h)
    scalar_constants()
    mask_scores(0)
    mask_scores(1)
    own_scores(0)
    own_scores(1)
    send_scores(0, 0)
    send_scores(0, 1)

    for r in range(R):
        peer = peer_of(r)
        qp, sp, qn, sn, lq, ls = ("%s%d" % (n, r) for n in ("qp", "sp", "qn", "sn", "lq", "ls"))
        wo, bo, bp = WO * r, BO * r, BP * r
        note(None, "ab%d" % r, (2 if r else 3) * bin(wide(r)).count("1"), [], [W(lq), W(ls)])

        def turn_scores():
            tr(W("t1", 0, 32), W("sc", 15, 512, 16))
            tr(W("t1", 32, 64), W("sc", SC0 + 15, SC0 + 512, 16))

        def turn_back():
            tr(W("wo", wo, wo + 32), W("t2", 0, 32))
            tr(W("wo", wo + 32 + NT, wo + 64 + NT), W("t2", 32, 64))

        chain = [turn_scores, lambda: cp(W("t2"), W("t1"), W("lrot", 0, 4)), turn_back]
        if r > 0:
            weave(chain, [lambda: None, lambda: ring_q(r, 1), lambda: ring_q(r, 2)])
        else:
            weave(chain, [lambda b=b: quant(blk("qe", b), blk("se", b), W("eb", 3 - b, 515 - b)) for b in range(4)])
        remote(peer, W(lq), W(qn, 0, CS), "ab%d" % r, wide(r), True)
        s0 = 0 if r else hx
        remote(peer, W(ls, s0, CS), W(sn, s0, CS), "ab%d" % r, wide(r))
        if r == 0:
            vector_constants()
        for b in range(4):
            mx(W("pb%d" % (4 + b), 0, C), blk("qe", b), blk("se", b), W(qp), W(sp))
        for b in range(4):
            mx(W("pb%d" % b, 0, CS), blk("qe", b), blk("se", b), W(lq), W(ls))

        def seg(name, t0, t1=None):
            return W(name, KW * t0, KW * (t0 + 1 if t1 is None else t1))

        def ends(name, t0, t1):
            return W(name, KW * t0 + KW - 1, KW * t1, KW)

        def least(k):
            scan(seg("mm", QT * k, QT * k + QT), W("rs"), seg("dd", QT * k, QT * k + QT), 0.0, A.max, A.min)

        def above(t0, t1):
            for t in range(t0, t1):
                ts(seg("fl", t), seg("mm", t), col("mm", KW * t + KW - 1), A.is_gt)

        def tally(t0, t1):
            scan(seg("cs", t0, t1), seg("kp", 0, t1 - t0), seg("fl", t0, t1), 0.0, A.mult, A.add)

        b0 = bo + 32 + 2 * NA
        nv = NT - NS

        def bcol(base, t):
            return base + t + (2 * NA if t >= HT else 0)

        for t in range(NT):
            act(seg("dd", t), W("wo", wo + 32 - V + t, wo + 32 + V + 1 + t), AF.Abs, bias=col("ap", NT * r + t), scale=-1.0)
        least(0)
        above(0, 2)
        least(1)
        above(2, QT)
        least(2)
        above(QT, 8)
        least(3)
        above(8, HT)
        tally(0, HT)
        for t in range(nv, NT):
            act(seg("jk", t), seg("mm", t), AF.Sign, bias=col("mm", KW * t + KW - 1), scale=-1.0, acc=col("nd", t))
        tt(W("bo", b0, b0 + HT), ends("cs", 0, HT), W("cb", 0, HT), A.add)
        ts(W("bo", b0 + HT, b0 + HT + NA), ends("cs", 0, NA), 2.0, A.mult, -2.0 * V, A.add)
        swap(r, "ay", W("bp", bp, bp + HT + NA), W("bo", b0, b0 + HT + NA))
        if nv > HT:
            above(HT, nv)
            tally(HT, nv)
            tt(W("bo", bcol(b0, HT), bcol(b0, nv)), ends("cs", HT, nv), W("cb", HT, nv), A.add)
        act(W("bo", b0 + HT + NA, b0 + HT + 2 * NA), W("nd", NT - NA, NT), bias=-2.0 * V, scale=-2.0)
        tt(W("bo", bcol(b0, nv), bcol(b0, NT)), W("cb", nv, NT), W("nd", nv, NT), A.subtract)
        swap(r, "az", W("bp", bp + BP - HT - NA, bp + BP), W("bo", b0 + HT + NA, b0 + 32))
        tr(W("t3"), W("bo", b0, b0 + 32))
        cp(W("t4"), W("t3"), W("lrot", 4, 8))
        tr(W("bo", bo, bo + 32), W("t4", 0, 32))
        tr(W("bo", bo + BO - 32, bo + BO), W("t4", 32, 64))
        tt(W("cd"), W("bo", bo, bo + BO), W("cdc", 2, 66), A.add, W("lc"))

        def mine(t):
            return bp + t + (NT if t >= HT else 0)

        def back(t0, t1):
            for t in range(t0, t1):
                act(seg("jk", t), W("cd", t, t + KW), AF.Sign, bias=col("bp", mine(t)), scale=-1.0 / 64, acc=col("ks", KW * t + KW - 1))

        def hits(t0, t1):
            for t in range(t0, t1):
                ts(seg("f2", t), W("cd", t, t + KW), 1.0 / 64, A.mult, col("bp", mine(t)), A.is_equal)

        def keys(t0, t1):
            for k in range(2):
                tt(W("kb", NT * k + t0, NT * k + t1), W("bp", mine(t0), mine(t0) + t1 - t0), W("ckb", NT * k + t0, NT * k + t1), A.add)

        def sums(t0, t1):
            scan(seg("ks", t0, t1), seg("kp", 0, t1 - t0), seg("f2", t0, t1), 0.0, A.mult, A.add)

        back(0, NA)
        hits(NA, HT)
        keys(0, HT)
        sums(NA, HT)
        back(NT - NA, NT)
        hits(HT, NT - NA)
        keys(HT, NT)
        sums(HT, NT - NA)
        for b in range(4):
            act(W("psb", PW * b, PW * b + CS), W("pb%d" % b, 0, CS), scale=0.5)
            act(W("psb", PW * b + CS, PW * b + CE), W("pb%d" % b, V, 2 * V), scale=0.5)
        tt(W("no", 0, NT), ends("ks", 0, NT), W("bp", bp + HT, bp + HT + NT), A.not_equal)
        scan(W("lo", 0, NT), W("no", 0, NT), W("kb", 0, NT), NONE, A.mult, A.max)
        scan(back_to_front(W("lo", NT, 2 * NT)), back_to_front(W("no", 0, NT)), back_to_front(W("kb", NT, 2 * NT)), NONE, A.mult, A.max)
        ts(W("zz", 0, 32), W("cz", 0, 32), col("lo", NT - 1), A.add, DEF, A.min)
        ts(W("zz", 96, 128), W("cz", 96, 128), col("lo", NT - 1), A.add, DEF, A.min)
        ts(W("zz", 32, 96), W("cz", 32, 96), col("lo", NT), A.add, DEF, A.min)
        tr(W("zt"), W("zz"))
        red(col("cl", 13), W("zt", 64, 128))
        red(col("cl", 12), W("zt", 0, 64))
        ts(W("fi", NT, 2 * NT), W("lo", NT, 2 * NT), col("cl", 13), A.min)
        ts(W("fi", 0, NT), W("lo", 0, NT), col("cl", 12), A.min)
        ts(W("lw", 0, 2 * NT), W("fi", 0, 2 * NT), 63, A.bitwise_and)
        tt(W("na", 0, 2 * NT), W("lw", 0, 2 * NT), W("cc", 0, 2 * NT), A.add)
        cp(W("off", 0, 2 * NT), W("na", 0, 2 * NT))
        nq, ns = "qp%d" % (r + 1), "sp%d" % (r + 1)

        def plane(b):
            return W("psb", PW * b, PW * b + CE)

        def part(name, b, h):
            return W(name, C * b + HC * h, C * b + HC * h + HC)

        def fetch(h, b):
            a = HC * h
            tt(W("yt", 4 * a + b, 4 * (a + HC), 4), plane(b), part("hb", b, h), A.add, W("off", HT * h, HT * h + HT))

        def layer(h):
            a = HC * h
            quant(W("qy", a, a + HC), W("sy", a, a + HC), W("yt", 4 * a, 4 * (a + HC)))
            for b in range(4):
                mx(W("pb%d" % b, 0, HC), blk("qw", b), blk("sw", b), W("qy", a, a + HC), W("sy", a, a + HC))
                act(part("rl", b, h), W("pb%d" % b, 0, HC), AF.Relu, scale=0.03125)

        def state(h, b0_, b1_):
            for b in range(b0_, b1_):
                tt(W("xt", 4 * HC * h + b, 4 * HC * (h + 1), 4), part("rl", b, h), W("pb%d" % (4 + b), HC * h, HC * h + HC), A.add)

        def pack(h):
            quant(W(nq, HC * h, HC * h + HC), W(ns, HC * h, HC * h + HC), W("xt", 4 * HC * h, 4 * HC * (h + 1)))

        for h in range(2):
            for b in range(4):
                hoff = W("off", NT + HT * h, NT + HT * h + HT)
                if (h, b) == (0, 1):
                    cp(part("hb", b, h), plane(b), hoff)
                else:
                    act(part("hb", b, h), plane(b), AF.Copy, ind=hoff)
        if r == R - 1:
            act(W("odt", 0, 2 * NT), W("na", 0, 2 * NT), bias=-float(V))
        for b in (1, 0, 2, 3):
            fetch(0, b)
        fetch(1, 0)
        layer(0)
        for b in range(1, 4):
            fetch(1, b)
        state(0, 0, 1)
        layer(1)
        state(0, 1, 4)
        if r == 0:
            quant(W("qv"), W("sv"), W("vt"))
        if r == R - 1:
            tt(W("odt", 0, 2 * NT), W("odt", 0, 2 * NT), W("cc", 0, 2 * NT), A.subtract)
            dma("s", T.od[:, 0:C], T.odt[:, 0:NT], [W("odt")], [])
            dma("s", T.od[:, C:2 * C], T.odt[:, NT:2 * NT], [W("odt")], [])
        pack(0)
        if r < R - 1:
            scores(r + 1, 0)
            state(1, 0, 2)
            mask_scores(0)
            state(1, 2, 3)
            own_scores(0)
            state(1, 3, 4)
            send_scores(r + 1, 0)
            pack(1)
            scores(r + 1, 1)
            ring_s(r + 1)
            ring_q(r + 1, 0)
            mask_scores(1)
            own_scores(1)
            send_scores(r + 1, 1)
        else:
            state(1, 0, 4)
            pack(1)

    qp, sp, qn, sn = "qp%d" % R, "sp%d" % R, "qn%d" % R, "sn%d" % R

    def store_scales(q, k):
        dma(q, T.osc[4 * k:4 * k + 4, :], T[sn][32 * k:32 * k + 4, 0:C], [W(sn, 0, C)], [])

    for h in range(2):
        a, b = HC * h, HC * h + HC
        picks(W(sn, a, b), W(sp), W("lnf", HT * h, HT * h + HT))
        pickq(W(qn, a, b), W(qp), W("lnf", HT * h, HT * h + HT))
        mx(W("pb%d" % h, 0, HC), W("qv"), W("sv"), W(qn, a, b), W(sn, a, b))
    dma("s", T.oc[:, 0:4 * HC], T[qn][:, 0:HC].bitcast(dt.uint8), [W(qn, 0, HC)], [])
    act(W("yo", 0, HC), W("pb0", 0, HC))
    dma("a", T.y[:, 0:HC], T.yo[:, 0:HC], [W("yo", 0, HC)], [])
    dma("s", T.oc[:, 4 * HC:4 * C], T[qn][:, HC:C].bitcast(dt.uint8), [W(qn, HC, C)], [])
    store_scales("s", 0)
    cp(W("yo", HC, C), W("pb1", 0, HC))
    for k in range(1, 4):
        store_scales("a", k)
    dma("s", T.y[:, HC:C], T.yo[:, HC:C], [W("yo", HC, C)], [])
    last = {events[e][0]: e for e in range(len(events))}
    for sem in sorted(count, key=lambda s: last.get(s, 0)):
        if all(known[q].get(sem, 0) < count[sem] for q in known):
            g.wait_ge(T.sem[sem], count[sem])
